import numpy as np, ml_dtypes
CORES = [8,136,40,168]
N = 4
BF = ml_dtypes.bfloat16
def gentries(a):
    return np.ascontiguousarray(a.reshape(8, 16, -1).transpose(0, 2, 1)).reshape(8, -1)
def gtable(e):
    e = np.asarray(e); return np.ascontiguousarray(e.reshape(8, -1, 16).transpose(0, 2, 1)).reshape(128, -1).astype(np.int32)
M, L, T, H, A, R = 896, 128, 3, 2048, 9, 512
W = M + L * T; NONE = 4095
def hashes(w, a):
    u = np.matmul(w.transpose(0, 2, 1), a) & 4095
    return (((u[:, 0] * u[:, 1]) >> 5) + u[:, 1]) & (H - 1)
def some(rng, n, tops):
    return (rng.random((N, 8, 16, n)) * rng.choice(np.array(tops), (N, 8, 1, n))).astype(np.int64)
def places(rng, sizes):
    v = np.zeros((N, 8, L), np.int64)
    for r in range(N):
        for g in range(8):
            pool = rng.permutation(M)[:int(sizes[r, g])]; v[r, g] = pool[rng.integers(0, len(pool), L)]
    return v
def flat(a):
    return np.ascontiguousarray(a.reshape(N, 128, -1)).astype(np.float32).astype(BF)
def pack(X, B, E, x, v, w):
    return {"nodes": flat(X), "book": flat(B), "kids": np.ascontiguousarray(E.reshape(N, 128, M)).astype(np.int32), "cand": flat(x),
            "spot": np.stack([gtable(a) for a in v]), "wts": flat(w)}
def setup_inputs(rng):
    X = some(rng, M, (48, 96, 160, 256)); B = some(rng, H, (96, 160, 256)); x = some(rng, L, (96, 192, 256))
    k = np.minimum(rng.integers(0, 17, (N, 8, 16, M)), rng.integers(0, 17, (N, 8, 16, M)))
    fill = rng.choice(np.array([0.3, 0.6, 0.9, 1.0]), (N, 8, 1, M))
    E = 4096 * k + np.where(rng.random((N, 8, 16, M)) < fill, rng.integers(0, M, (N, 8, 16, M)), NONE)
    v = places(rng, rng.choice(np.array([8, 32, 128, M]), (N, 8)))
    return pack(X, B, E, x, v, rng.integers(0, 16, (N, 8, 16, 2)))
def setup_inputs_spread(rng):
    X = (np.exp2(8 * rng.random((N, 8, 1, M))) * rng.random((N, 8, 16, M))).astype(np.int64)
    x = (np.exp2(8 * rng.random((N, 8, 1, L))) * rng.random((N, 8, 16, L))).astype(np.int64); B = rng.integers(0, 256, (N, 8, 16, H))
    E = 4096 * rng.integers(0, 17, (N, 8, 16, M)) + np.where(rng.random((N, 8, 16, M)) < rng.random((N, 8, 1, M)), rng.integers(0, M, (N, 8, 16, M)), NONE)
    v = np.minimum((M * rng.random((N, 8, L)) ** 3).astype(np.int64), M - 1); w = np.minimum((16 * rng.random((N, 8, 16, 2)) ** 2).astype(np.int64), 15)
    return pack(X, B, E, x, v, w)
def setup_inputs_ends(rng):
    X = 255 * rng.integers(0, 2, (N, 8, 16, M)); B = 255 * rng.integers(0, 2, (N, 8, 16, H)); x = 255 * rng.integers(0, 2, (N, 8, 16, L))
    a = rng.random((N, 8, 1, L)); x = np.where(a < 0.15, 0, np.where(a < 0.4, 255, x))
    X[..., 0] = 0; X[..., M - 1] = 255
    w = 15 * rng.integers(0, 2, (N, 8, 16, 2)); w[:, ::2, 13] = 15; w[:, ::2, 14] = 1; w[:, ::2, 15] = 15; w[:, 7] = 15
    E = 69631 * rng.integers(0, 2, (N, 8, 16, M)); o = rng.random(E.shape)
    E = np.where(o < 0.35, rng.choice(np.array([65536, M - 1, M - 1 + 65536]), E.shape), E)
    E = np.where(o < 0.1, rng.integers(1, M - 16, E.shape) + 65536 * rng.integers(0, 2, E.shape), E)
    E[..., M - 1] = 69631 * rng.integers(0, 2, (N, 8, 16)); E[:, :, 15, M - 1] = M - 1 + 65536; low = rng.integers(0, 8, (N, 8))
    E[:, :, :15, M - 2] = 0; E[:, :, 15, M - 2] = 69631
    for j in range(1, T): E[:, :, :, M - 2 - j] = 65536 + M - 1 - j
    E[:, :, :15, M - 2 - T] = 69631; E[:, :, 15, M - 2 - T] = 0
    v = np.where(rng.random((N, 8, L)) < 0.68, (M - 1) * rng.integers(0, 2, (N, 8, L)), rng.integers(1, M - 16, (N, 8, L)))
    v[:, :, L - 1] = M - 1 - T; x[..., L - 1] = 255
    v[:, :, L - 17] = M - 1; x[..., L - 17] = 255
    v[:, :, L - 33] = M - 2 - T; x[..., L - 33] = 255
    v[:, :, L - 2] = M - 1; x[:, ::2, :, L - 2] = 0; x[:, ::2, 14:, L - 2] = 255; x[:, ::2, 13, L - 2] = 1
    s = rng.integers(0, 2, (N, 8)); s[:, 7] = 1; s[:, 1] = 0
    for r in range(N):
        h = hashes(w[r], np.full((8, 16, 1), 255))[:, 0]
        for g in range(8):
            B[r, g, :, h[g]] = 255 * s[r, g]; E[r, g, low[r, g], M - 1] = 65536
    return pack(X, B, E, x, v, w)
def setup_inputs_corners(rng):
    X = some(rng, M, (2, 64, 256)); B = some(rng, H, (2, 128, 256))
    kind = rng.integers(0, 9, (N, 8, 1, M)); kind[..., 5:6 + T] = 4
    own = np.arange(M); one = rng.integers(0, 16, (N, 8, 1, M)); line = np.arange(16)[:, None]
    c = rng.integers(0, M, (N, 8, 16, M))
    c = np.where(kind == 3, own, np.where(kind == 4, (own + 1) % M, np.where(kind == 5, 0, np.where(kind == 6, M - 1, c))))
    hide = (kind == 0) | ((kind == 2) & (line != one)) | ((kind == 7) & (line == one)) | ((kind == 8) & (rng.random(c.shape) < 0.5))
    m = rng.integers(0, 4, (N, 8, 1, M)); m = np.where(kind == 4, 1, m)
    k = np.where(m == 0, 0, np.where(m == 1, 16, np.where(m == 2, 15, rng.integers(0, 17, c.shape))))
    E = 4096 * k + np.where(hide, NONE, c)
    v = rng.integers(0, M, (N, 8, L)); w = rng.integers(0, 16, (N, 8, 16, 2))
    for r in range(N):
        o = rng.permutation(8); q = rng.permutation(M)
        v[r, o[0]] = 0; v[r, o[1]] = M - 1; v[r, o[2]] = q[:L]; v[r, o[3]] = rng.permutation(np.repeat(q[:L // 2], 2))
        v[r, o[4]] = rng.choice(np.array([5, 0, M - 1, 6]), L); v[r, o[5], ::2] = 5; v[r, o[5], L - 1] = 5
        b = rng.permutation(8)
        w[r, b[0]] = 0; w[r, b[1]] = 15; w[r, b[2], 1:] = 0; w[r, b[2], 0] = 15; w[r, b[3], :15] = 0; w[r, b[3], 15] = 15; w[r, b[4], :, 0] = 0; w[r, b[5], :, 1] = 0
    d = rng.integers(0, 4, (N, 8, 1, L)); x = some(rng, L, (64, 256))
    x = np.where(d == 0, 0, np.where(d == 1, 255, np.where(d == 2, np.take_along_axis(X, v[:, :, None, :], 3), x)))
    return pack(X, B, E, x, v, w)
def full(rng, X, B, E, x, v, r, late):
    n = T - 1 if late else 0; half = rng.permutation(8)
    for g in range(8):
        u = rng.permutation(M)[:L * T].reshape(T, L); e = E[r, g]; v[r, g] = u[0]
        for j in range(n): e[:, u[j]] = 65536 + u[j + 1][None, :]
        if half[g] < 4:
            e[:, u[n]] = NONE + 4096 * rng.integers(0, 17, (16, L))
        else:
            X[r, g] = rng.integers(0, 8, (16, M)); x[r, g] = rng.integers(8, 24, (16, L)); B[r, g] = rng.integers(24, 256, (16, H))
            e[:, u[n]] = rng.integers(0, M, (16, L)) + 4096 * rng.integers(0, 16, (16, L))
def setup_inputs_crowd(rng):
    X = some(rng, M, (16, 64, 128)); B = some(rng, H, (160, 256)); x = np.minimum(some(rng, L, (128, 256)) + rng.integers(0, 64, (N, 8, 1, L)), 255)
    k = rng.integers(0, 17, (N, 8, 16, M)) * (rng.random((N, 8, 16, M)) < 0.3); fill = rng.choice(np.array([0.5, 1.0]), (N, 8, 1, M))
    E = 4096 * k + np.where(rng.random((N, 8, 16, M)) < fill, rng.integers(0, M, (N, 8, 16, M)), NONE)
    v = places(rng, rng.choice(np.array([1, 2, 3, 16]), (N, 8))); v[:, 0] = 0; v[:, 7] = M - 1
    o = rng.permutation(N); full(rng, X, B, E, x, v, int(o[0]), False); full(rng, X, B, E, x, v, int(o[1]), True)
    return pack(X, B, E, x, v, rng.integers(0, 16, (N, 8, 16, 2)))
def setup_inputs_ties(rng):
    X = 100 + rng.integers(0, 3, (N, 8, 16, M)); x = 100 + rng.integers(0, 3, (N, 8, 16, L)); B = rng.integers(0, 3, (N, 8, 16, H))
    c = rng.integers(0, M, (N, 8, 16, M)); c[:, ::2, 8:] = c[:, ::2, :8]
    E = 4096 * rng.integers(8, 15, c.shape) + np.where(rng.random(c.shape) < 0.8, c, NONE)
    v = places(rng, rng.choice(np.array([4, 16, 64, M]), (N, 8)))
    return pack(X, B, E, x, v, rng.integers(0, 16, (N, 8, 16, 2)))
def check_inputs(d):
    bad = []
    for k, lo, hi in (("nodes", 0, 255), ("book", 0, 255), ("kids", 0, 69631), ("cand", 0, 255), ("spot", 0, M - 1), ("wts", 0, 15)):
        a = np.asarray(d[k]).astype(np.float32)
        if not (np.min(a) >= lo and np.max(a) <= hi and np.all(a == np.floor(a))): bad.append("range of " + k)
    c = np.asarray(d["kids"]).astype(np.int64) & 4095
    if np.any((c >= M) & (c != NONE)): bad.append("children in kids")
    return bad
def reference(nodes, book, kids, cand, spot, wts):
    X = np.zeros((N, 8, 16, W), np.int64); X[..., :M] = nodes.astype(np.float32).astype(np.int64).reshape(N, 8, 16, M)
    E = np.full((N, 8, 16, W), NONE, np.int64); E[..., :M] = kids.astype(np.int64).reshape(N, 8, 16, M)
    B = book.astype(np.float32).astype(np.int64).reshape(N, 8, 16, H); w = wts.astype(np.float32).astype(np.int64).reshape(N, 8, 16, 2)
    xs = cand.astype(np.float32).astype(np.int64).reshape(N, 8, 16, L).copy(); vs = np.stack([gentries(a) for a in spot]).astype(np.int64)
    lane = np.arange(L); p = lane & 15; gr = np.arange(8)[:, None]
    for t in range(T):
        for r in range(N):
            x, v, q = xs[r], vs[r], (r + 1 + t % (N - 1)) % N
            ev = np.take_along_axis(E[r], v[:, None, :], 2)
            c = ev & 4095; thr = ev >> 12; filled = c != NONE
            xc = np.take_along_axis(X[r], np.where(filled, c, 0).reshape(8, 1, 16 * L), 2).reshape(8, 16, 16, L)
            dif = np.abs(x[:, :, None, :] - xc); fd = dif.reshape(8, 16, 16 * L)
            bc = np.take_along_axis(B[r], hashes(w[r], fd)[:, None, :], 2)
            s = np.add.reduce((bc >= fd).astype(np.int64), axis=1).reshape(8, 16, L)
            over = np.add.reduce((x[:, :, None, :] >= xc).astype(np.int64), axis=1)
            cap = filled & (over >= A) & (s > thr); stay = filled & ~cap
            go = stay[:, p, lane]
            best = np.argmax(np.where(stay, s, -1), axis=1)
            down = np.take_along_axis(c, best[:, None, :], 1)[:, 0]
            first = np.full((8, W), L); np.minimum.at(first, (gr, v), np.where(go, L, lane[None, :]))
            win = ~go & (first[gr, v] == lane[None, :]); wb = win[:, None, :]
            z = np.abs(np.take_along_axis(X[r], v[:, None, :], 2) - x)
            y = np.take_along_axis(B[q], hashes(w[q], z)[:, None, :], 2)
            n = M + L * t + lane
            X[r][:, :, M + L * t:M + L * t + L] = np.where(wb, x, 0)
            E[r][:, :, M + L * t:M + L * t + L] = np.where(wb & cap, c + 4096 * s, NONE)
            col = np.where(cap, NONE, ev); col[:, p, lane] = n[None, :] + 4096 * np.max(np.where(cap, s, 0), axis=1)
            gi, li = np.nonzero(win)
            E[r][gi, :, v[gi, li]] = col[gi, :, li]
            x = np.where(wb, np.abs(x - y), x)
            back = np.add.reduce(w[r][:, :, 0:1] * x, axis=1) & (R - 1)
            xs[r] = x; vs[r] = np.where(win, back, np.where(go, down, v))
    return {"ykids": E.reshape(N, 128, W).astype(np.float32), "ynodes": np.ascontiguousarray(X[..., M:]).reshape(N, 128, L * T).astype(np.float32).astype(BF),
            "ycand": xs.reshape(N, 128, L).astype(np.float32).astype(BF), "yspot": np.stack([gtable(a) for a in vs]).astype(np.float32)}

@@ -1,0 +1,504 @@
+from concourse.mybir import AluOpType as A, ActivationFunctionType as F
+
+M, L, STEPS, H, R, NB = 896, 128, 3, 2048, 512, 4
+XW = 1296
+SBANKS = (2, 3)
+XS = (3,)
+
+BF, F32, I32, U16 = "bfloat16", "float32", "int32", "uint16"
+_S = {
+    "spi": (8, I32), "E": (128 + 1280, I32), "EF": (128 + 1280, F32), "X": (XW, BF), "bk": (3 * H, BF), "XX": (2 * L, BF),
+    "wt": (2, BF), "wl0": (2, BF), "wl1": (2, BF), "wl2": (2, BF),
+    "qs": (8 * STEPS, U16), "ql": (8 * STEPS, U16), "ys": (L * STEPS, BF), "yl": (L * STEPS, BF),
+    "one": (128, BF), "zer": (256, BF), "pk": (128, I32), "Id": (128, BF), "nId": (128, BF), "IF": (256, F32), "JJ": (256, BF), "CA": (256, BF),
+    "BD0": (128, BF), "BD": (128, BF), "BDf": (8, F32), "P": (128, BF), "Pb": (128, BF), "P4": (128, F32), "P128": (128, BF), "TPm": (128, BF),
+    "NEG": (256, BF), "I4": (128, BF), "Iq": (128, BF), "I14": (256, BF), "nIh": (128, BF), "BDq": (128, BF), "BD16": (128, BF), "CH2": (16, BF),
+    "RB": (16, BF), "RBh": (16, BF), "WO": (128, BF), "WI": (128, BF), "CK": (256, BF), "Ex": (2048, BF), "Mh": (128, BF), "W": (16, BF), "Wz": (48, BF),
+    "LW": (2048, BF), "lwo": (2, U16), "wrep": (16, BF), "chp": (8, BF),
+    "ni": (128, F32), "Pn": (128, F32), "pt": (128, I32), "ptb": (256, BF), "lowb": (128, BF), "hib": (16, F32), "CODE": (1280, BF),
+    "lst": (16, U16), "e2": (16, F32), "BW": (16, F32), "BB": (16, F32),
+    "Ci": (128, I32), "C16": (128, U16), "XC": (2048, BF), "D": (2048, BF), "xT": (128, BF), "XV": (128, BF), "z": (128, BF), "zh": (128, F32),
+    "Ui": (256, I32), "U2": (256, I32), "h1": (128, I32), "h2": (128, I32), "hf": (128, F32), "H16": (128, U16), "BC": (2048, BF),
+    "CG": (128, BF), "CGm": (256, BF), "EQ": (1024, BF), "evf": (128, F32), "d4": (128, BF), "fe": (128, BF), "d4P": (128, BF), "feP": (128, BF),
+    "Cf": (128, F32), "AA": (256, F32), "evP": (128, F32), "Kc": (256, F32), "ov": (256, F32), "xm": (256, BF),
+    "wr": (128, BF), "wd": (128, BF), "cap": (128, BF), "nc": (128, F32), "mk": (128, F32), "sc": (128, F32), "zc": (128, F32),
+    "scap": (128, BF), "scs": (128, F32), "sp": (128, BF), "wP": (128, BF), "wL": (128, BF),
+    "mm": (256, F32), "VC": (128, F32), "n1": (128, F32), "n2": (128, F32),
+    "i8": (128, I32), "f8": (128, F32),
+}
+SCRATCH = {k: ("sbuf", [128, w], d) for k, (w, d) in _S.items()}
+for _k in ("OV", "IN"):
+    SCRATCH[_k] = ("sbuf", [128, 8, 256], BF)
+for _k in ("PD0", "PD1", "PD2", "PD3", "PB4", "PB5", "PB6", "PB7"):
+    SCRATCH[_k] = ("psum", [128, 512], F32)
+_I8 = {"uz": (0, 16), "uz2": (16, 16), "hz1": (32, 8), "hz2": (40, 8), "bk1": (48, 8), "bk2": (56, 8), "ch1": (64, 8), "ch2": (72, 8),
+       "ip": (80, 1), "p15": (84, 1), "mi": (88, 1), "g8": (96, 8)}
+_F8 = {"hz": (0, 8), "ch3": (8, 8), "ch4": (16, 8), "il": (24, 8), "c128": (32, 8), "e1": (40, 16), "lwi": (56, 1), "colk": (60, 1), "m0": (64, 1),
+       "m1": (68, 1), "lwf": (72, 1)}
+SLICED = set("Ex W JJ I14 CH2 RB RBh CK CA ptb zh zc sp IF WI CGm Wz CODE IN0 IN1 IN2 IN3".split())
+DMAS = ["spi", "E", "x", "X", "wt", "bk0", "bk1", "bk2", "out"]
+SEMAPHORES = (["sV", "sS", "sP", "sG", "wloc", "wrem"] + ["d_" + k for k in DMAS]
+              + [k + str(t) for k in ("qa", "qo", "ya", "yo") for t in range(STEPS)])
+
+
+def rank_program(g, core, T, topo):
+    rank = T.rank_of(core)
+    if rank is None:
+        return
+    Q = {"V": g.vector, "S": g.scalar, "P": g.tensor, "G": g, "Y": g.sync}
+    cnt = {k: 0 for k in "VSPG"}
+    known = {k: {} for k in Q}
+    snap = {}
+    lastw, readers, banks = {}, {}, {}
+    B = {k: T[k] for k in SCRATCH}
+
+    def sm(k, a=0, b=None):
+        buf, (o, w) = ("i8", _I8[k]) if k in _I8 else ("f8", _F8[k])
+        return B[buf][:, o + a:o + (w if b is None else b)]
+
+    def wait(eng, toks):
+        best = {}
+        for s, v in toks:
+            if known[eng].get(s, 0) < v:
+                best[s] = max(best.get(s, 0), v)
+        for s, v in sorted(best.items(), key=lambda a: -len(snap.get(a, ()))):
+            if known[eng].get(s, 0) >= v:
+                continue
+            Q[eng].wait_ge(T.sem[s], v)
+            known[eng][s] = v
+            for a, b in snap.get((s, v), {}).items():
+                known[eng][a] = max(known[eng].get(a, 0), b)
+
+    def deps(eng, rd, wr):
+        toks = []
+        for k in rd:
+            if k in lastw:
+                toks.append(lastw[k][1])
+        for k in wr:
+            if k in lastw and (lastw[k][0] != eng or (eng != "P" and k not in SLICED)):
+                toks.append(lastw[k][1])
+            for e, t in readers.get(k, {}).items():
+                if e != eng or eng != "P":
+                    toks.append(t)
+        for k in list(rd) + list(wr):
+            if k[:2] in ("PD", "PB"):
+                for e, t in banks.get(k[:3], {}).items():
+                    if e != eng:
+                        toks.append(t)
+        return toks
+
+    def done(eng, tok, rd, wr):
+        snap[tok] = dict(known[eng])
+        for k in wr:
+            lastw[k] = (eng, tok)
+            readers[k] = {}
+        for k in rd:
+            readers.setdefault(k, {})[eng] = tok
+        for k in list(rd) + list(wr):
+            if k[:2] in ("PD", "PB"):
+                banks.setdefault(k[:3], {})[eng] = tok
+
+    def op(eng, rd, wr, fn):
+        rd, wr = rd.split(), wr.split()
+        wait(eng, deps(eng, rd, wr))
+        i = fn()
+        cnt[eng] += 1
+        i.then_inc(T.sem["s" + eng], 1)
+        done(eng, ("s" + eng, cnt[eng]), rd, wr)
+
+    dcount = {}
+
+    def dma(eng, rd, wr, sem, out, in_):
+        rd, wr = rd.split(), wr.split()
+        wait(eng, deps(eng, rd, wr))
+        Q[eng].dma_start(out, in_).then_inc(T.sem["d_" + sem], 16)
+        dcount[sem] = dcount.get(sem, 0) + 16
+        tok = ("d_" + sem, dcount[sem])
+        snap[tok] = dict(known[eng])
+        for k in wr:
+            lastw[k] = ("dma", tok)
+            readers[k] = {}
+        for k in rd:
+            readers.setdefault(k, {})["dma" + sem] = tok
+
+    V, S, PE = g.vector, g.scalar, g.tensor
+
+    def tt(rd, wr, out, a, b, o):
+        op("V", rd, wr, lambda: V.tensor_tensor(out, a, b, o))
+
+    def ts(rd, wr, out, a, s1, s2, o0, o1=None):
+        if o1 is None:
+            op("V", rd, wr, lambda: V.tensor_scalar(out, a, s1, s2, o0))
+        else:
+            op("V", rd, wr, lambda: V.tensor_scalar(out, a, s1, s2, o0, o1))
+
+    def cp(rd, wr, out, a):
+        op("V", rd, wr, lambda: V.tensor_copy(out, a))
+
+    def act(rd, wr, out, a, f, **kw):
+        op("S", rd, wr, lambda: S.activation(out, a, f, **kw))
+
+    def mms(rd, wr, lst):
+        def go():
+            i = None
+            for out, l, r, st, sp in lst:
+                i = PE.matmul(out, l, r, st, sp)
+            return i
+        op("P", rd, wr, go)
+
+    def memset(wr, ap, c):
+        op("V", "", wr, lambda: V.memset(ap, c))
+
+    nx, x = B["XX"][:, 0:L], B["XX"][:, L:2 * L]
+    dma("Y", "", "spi", "spi", B["spi"][:], T.spot[:])
+    dma("Y", "", "E", "E", B["E"][:, 128:128 + M], T.kids[:])
+    dma("S", "", "wt", "wt", B["wt"][:], T.wts[:])
+    dma("S", "", "x", "x", x, T.cand[:])
+    dma("S", "", "X", "X", B["X"][:, 0:M], T.nodes[:])
+    for j in range(3):
+        dma("Y", "", "bk%d" % j, "bk%d" % j, B["bk"][:, H * j:H * j + H], T.book[:])
+
+    memset("one", B["one"][:], 1.0)
+    memset("zer", B["zer"][:], 0.0)
+    op("G", "one", "Id", lambda: g.affine_select(B["Id"][:], B["one"][:], [[-1, 128]], A.is_equal, 0.0, 0, 1))
+    op("G", "one", "BD0", lambda: g.affine_select(B["BD0"][:], B["one"][:], [[-16, 8], [0, 16]], A.is_ge, 0.0, 0, 1))
+    op("G", "BD0", "BD", lambda: g.affine_select(B["BD"][:], B["BD0"][:], [[16, 8], [0, 16]], A.is_ge, 0.0, 15, -1))
+    op("G", "", "pk", lambda: g.iota(B["pk"][:], [[0, 8], [-1, 16]], 16, 1))
+    op("G", "", "ip", lambda: g.iota(sm("ip"), [[0, 1]], 0, 1))
+    op("G", "", "g8", lambda: g.iota(sm("g8"), [[0, 8]], 0, 1))
+    wait("G", deps("G", ["wt"], []))
+    for j in range(NB - 1):
+        d = T.cores[(rank - 1 - j) % NB]
+        rid, pid = topo.addr(d, core)
+        g.remote_dma(B["wl%d" % j][:], B["wt"][:], T.sem.wrem, T.sem.wloc, pid, rid, topo.mask(core, d))
+    neng = len(topo.engines(core, T.cores[(rank + 1) % NB]))
+    for j in range(NB - 1):
+        lastw["wl%d" % j] = ("rem", ("wrem", neng * (NB - 1)))
+    op("G", "zer", "NEG", lambda: g.affine_select(B["NEG"][:], B["zer"][:], [[0, 2], [1, 128]], A.is_gt, -100.0, 0, -1))
+    op("G", "", "ni", lambda: g.iota(B["ni"][:], [[1, 128]], M, 0, allow_small_or_imprecise_dtypes=True))
+    op("G", "", "LW", lambda: g.iota(B["LW"][:], [[0, 2048]], 0, 0, allow_small_or_imprecise_dtypes=True))
+
+    cp("spi", "lst", B["lst"][:, 8:16], B["spi"][:])
+    cp("spi", "e2", B["e2"][:, 8:16], B["spi"][:])
+    memset("Xz", B["X"][:, M:XW], 0.0)
+    memset("ptb0", B["ptb"][:], 0.0)
+    memset("Mh", B["Mh"][:], 1.0)
+    memset("Mh", B["Mh"][:, 0:128:16], 0.0)
+    memset("IF", B["IF"][:, 128:256], 0.0)
+    memset("CA", B["CA"][:, 0:128], -2.0)
+    memset("CA", B["CA"][:, 128:256], 0.0)
+    for j in range(2):
+        memset("CK", B["CK"][:, 128 * j:128 * j + 128], (2048.0, 0.0625)[j])
+    bd8 = B["BD"][:, 0:128:16]
+    ts("Id", "nId", B["nId"][:], B["Id"][:], -1.0, None, A.mult)
+    mms("x Id", "PB7x", [(B["PB7"][:, 256:384], x, B["Id"][:], True, True)])
+    act("PB7x", "xT", B["xT"][:], B["PB7"][:, 256:384], F.Copy)
+    EXR = "Ex"
+    for k in range(16):
+        if k % 3 == 2:
+            act("Id", "Ex%d" % k, B["Ex"][:, k:2048:16], B["Id"][:], F.Copy)
+            EXR += " Ex%d" % k
+        else:
+            cp("Id", "Ex", B["Ex"][:, k:2048:16], B["Id"][:])
+    for u in range(2):
+        ts("BD wt", "W", B["W"][:, 8 * u:8 * u + 8], bd8, B["wt"][:, u:u + 1], None, A.mult)
+    ts("pk", "Ci", B["Ci"][:], B["pk"][:], 15, None, A.bitwise_and)
+    ts("Ci", "P", B["P"][:], B["Ci"][:], 0, None, A.is_equal)
+    cp("Id", "IF", B["IF"][:, 0:128], B["Id"][:])
+    cp("BD", "BDf", B["BDf"][:], bd8)
+    ts("ip", "p15", sm("p15"), sm("ip"), 15, None, A.bitwise_and)
+    ts("p15", "colk", sm("colk"), sm("p15"), -2048.0, 30720.0, A.mult, A.add)
+    ts("P", "Pb", B["Pb"][:], B["P"][:], -1.0, 1.0, A.mult, A.add)
+    ts("P", "TPm", B["TPm"][:], B["P"][:], 1000.0, -1000.0, A.mult, A.add)
+    ts("Pb", "P4", B["P4"][:], B["Pb"][:], 4095.0, None, A.mult)
+    for k, src, f in (("P128", "P", 128.0), ("I4", "Id", 4096.0), ("Iq", "Id", 1.0 / 4096), ("nIh", "Id", -0.5), ("BDq", "BD", 1.0 / 4096),
+                      ("BD16", "BD", -16.0)):
+        ts(src, k, B[k][:], B[src][:], f, None, A.mult)
+    for j in range(2):
+        ts("Id", "I14", B["I14"][:, 128 * j:128 * j + 128], B["Id"][:], (-16384.0, 0.0)[j], None, A.mult)
+        ts("Id", "JJ", B["JJ"][:, 128 * j:128 * j + 128], B["Id"][:], (256.0, -256.0)[j], None, A.mult)
+        cp("BD", "CH2", B["CH2"][:, 8 * j:8 * j + 8], bd8)
+        ts("BD", "RB", B["RB"][:, 8 * j:8 * j + 8], bd8, (32768.0, 1.0)[j], None, A.mult)
+        ts("BD", "RBh", B["RBh"][:, 8 * j:8 * j + 8], bd8, (16384.0, 0.5)[j], None, A.mult)
+    pt = B["pt"]
+    for b in range(7):
+        ts("g8", "pt%d" % b, pt[:, b:128:16], sm("g8"), b, 1, A.logical_shift_right, A.bitwise_and)
+    for b in range(7):
+        ts("ptb0 pt%d" % b, "ptb", B["ptb"][:, b:128:16], pt[:, b:128:16], 2.0, -1.0, A.mult, A.add)
+    for b in range(7, 11):
+        ts("pt%d" % (b - 7), "ptb", B["ptb"][:, 128 + b:256:16], pt[:, b - 7:128:16], 2.0, -1.0, A.mult, A.add)
+    mms("ptb Id", "PB7c", [(B["PB7"][:, 256:384], B["ptb"][:, 0:128], B["Id"][:], True, True),
+                           (B["PB7"][:, 384:400], B["ptb"][:, 128:256], B["Id"][:, 0:16], True, True)])
+    act("PB7c", "hib", B["hib"][:], B["PB7"][:, 384:400], F.Copy)
+    act("PB7c", "lowb", B["lowb"][:], B["PB7"][:, 256:384], F.Copy)
+    for h in range(10):
+        act("lowb hib", "CODE", B["CODE"][:, 128 * h:128 * h + 128], B["lowb"][:], F.Identity, bias=B["hib"][:, h:h + 1])
+    ts("ip", "mi", sm("mi"), sm("ip"), 4, 1, A.logical_shift_right, A.bitwise_and)
+    cp("mi", "m1", sm("m1"), sm("mi"))
+    ts("m1", "m0", sm("m0"), sm("m1"), -1.0, 1.0, A.mult, A.add)
+    cp("ip", "lwi", sm("lwi"), sm("ip"))
+    ts("BD lwi", "chp", B["chp"][:], bd8, sm("lwi"), None, A.mult)
+    mms("P chp", "PB7i", [(B["PB7"][:, 152:160], B["P"][:], B["chp"][:], True, True)])
+    cp("PB7i", "il", sm("il"), B["PB7"][:, 152:160])
+    ts("il", "c128", sm("c128"), sm("il"), -1.0, 128.0, A.mult, A.add)
+    cp("il", "BBa", B["BB"][:, 0:8], sm("il"))
+
+    def late_consts():
+        tt("P ni", "Pn", B["Pn"][:], B["P"][:], B["ni"][:], A.mult)
+        ts("p15 lwi", "lwf", sm("lwf"), sm("p15"), 128.0, sm("lwi"), A.mult, A.add)
+        cp("lwf", "lwo", B["lwo"][:, 0:1], sm("lwf"))
+        ts("one wt", "wrep", B["wrep"][:], B["one"][:, 0:16], B["wt"][:, 0:1], None, A.mult)
+        op("V", "lwo wrep LW", "LW", lambda: V.tensor_copy(B["LW"][:].indirect(B["lwo"][:, 0:1]), B["wrep"][:]))
+
+    PD = [B["PD%d" % b] for b in range(4)]
+    U, KS, PB6, PM = B["PB4"], B["PB5"], B["PB6"], B["PB7"]
+    v16, vf = B["lst"][:, 8:16], B["e2"][:, 8:16]
+    sb = list(SBANKS)
+    vbk = [b for b in range(4) if b not in sb]
+    vb = [b for b in range(4) if b not in XS]
+    order = vb[:1] + list(XS) + vb[1:]
+    ch = [slice(512 * b, 512 * b + 512) for b in range(4)]
+    c32 = [slice(32 * b, 32 * b + 32) for b in range(4)]
+
+    def newcols(t):
+        tt("PB5n AAa", "mma", B["mm"][:, 0:128], KS[:, 0:128], B["AA"][:, 0:128], A.mult)
+        tt("PB5n mma", "n1", B["n1"][:], KS[:, 128:256], B["mm"][:, 0:128], A.add)
+        tt("PB5n n1", "n2", B["n2"][:], KS[:, 256:384], B["n1"][:], A.mult)
+        k = "EF" if t == STEPS - 1 else "E"
+        c = 128 + M + L * t
+        ts("n2", k + str(t), B[k][:, c:c + L], B["n2"][:], 4095.0, None, A.add)
+
+    for t in range(STEPS):
+        last = t == STEPS - 1
+        wg = M + L * max(0, t - 1)
+        ER = "E " + " ".join("E%d" % j for j in range(t - 1))
+        qb = (rank + 1 + t) % NB
+        qf = (rank - 1 - t) % NB
+        ts(ER + " lst", "Ci", B["Ci"][:], B["E"][:, 128:128 + wg].indirect(v16), 4095, None, A.bitwise_and)
+        ts("Ci", "C16", B["C16"][:], B["Ci"][:], 1280.0, None, A.min)
+        act("X Xz lst", "XV", B["XV"][:], B["X"][:].indirect(v16), F.Copy)
+        for b in order:
+            mms("%s xT" % EXR, "PD%d" % b, [(PD[b][:], B["xT"][:], B["Ex"][:, ch[b]], True, False)])
+
+        def diff(b):
+            mms("nId XC%d" % b, "PD%d" % b, [(PD[b][:], B["nId"][:], B["XC"][:, ch[b]], False, True)])
+
+        def hashsum(b):
+            mms("D%d W" % b, "PB4u", [(U[c32[b], k:256:16], B["D"][:, 512 * b + k:512 * b + 512:16], B["W"][:], True, True) for k in range(16)])
+
+        for b in XS:
+            act("X Xz C16", "XC%d" % b, B["XC"][:, ch[b]], B["X"][:].indirect(B["C16"][:, c32[b]]), F.Copy)
+        mms("XV x Id nId", "PB7z", [(PM[:, 0:128], B["Id"][:], B["XV"][:], True, False), (PM[:, 0:128], B["nId"][:], x, False, True)])
+        act("PB7z", "z", B["z"][:], PM[:, 0:128], F.Abs)
+        if t == 0:
+            for j in range(3):
+                for u in range(2):
+                    ts("BD wl%d" % j, "Wz", B["Wz"][:, 16 * j + 8 * u:16 * j + 8 * u + 8], bd8, B["wl%d" % j][:, u:u + 1], None, A.mult)
+        for b in vb:
+            cp("X Xz C16", "XC%d" % b, B["XC"][:, ch[b]], B["X"][:].indirect(B["C16"][:, c32[b]]))
+        diff(order[0])
+        mms("z Wz", "PB7u", [(PM[:, 128:144], B["z"][:], B["Wz"][:, 16 * t:16 * t + 16], True, True)])
+        for b in order[1:3]:
+            diff(b)
+        act("CODE lst", "CG", B["CG"][:], B["CODE"][:].indirect(v16), F.Copy)
+        for n, b in enumerate(order):
+            if n == 1:
+                diff(order[3])
+            act("PD%d" % b, "D%d" % b, B["D"][:, ch[b]], PD[b][:], F.Abs)
+            if n < 3:
+                hashsum(b)
+        cp("PB7u", "uz", sm("uz"), PM[:, 128:144])
+        ts("uz", "uz2", sm("uz2"), sm("uz"), 4095, None, A.bitwise_and)
+        tt("uz2", "hz1", sm("hz1"), sm("uz2", 0, 8), sm("uz2", 8, 16), A.mult)
+        ts("hz1", "hz2", sm("hz2"), sm("hz1"), 5, H - 1, A.logical_shift_right, A.bitwise_and)
+        if t:
+            tt("hz2 uz2", "hz", sm("hz"), sm("hz2"), sm("uz2", 8, 16), A.add)
+        else:
+            tt("hz2 uz2", "hz1", sm("hz1"), sm("hz2"), sm("uz2", 8, 16), A.add)
+            ts("hz1", "hz2", sm("hz2"), sm("hz1"), H - 1, None, A.bitwise_and)
+            cp("hz2", "hz", sm("hz"), sm("hz2"))
+        for k in range(8):
+            ts("P hz", "zh", B["zh"][:, 16 * k:16 * k + 16], B["P"][:, 0:16], sm("hz", k, k + 1), None, A.mult)
+        mms("zh BDf", "PB7q", [(PM[:, 144:152], B["zh"][:], B["BDf"][:], True, True)])
+        hashsum(order[3])
+        ts("Ci", "fe", B["fe"][:], B["Ci"][:], 4095.0, 128.0, A.is_ge, A.mult)
+        ts("Ci colk", "Cf", B["Cf"][:], B["Ci"][:], sm("colk"), None, A.add)
+        cp("PB7q", "qs%d" % t, B["qs"][:, 8 * t:8 * t + 8], PM[:, 144:152])
+        wait("G", deps("G", ["qs%d" % t], []))
+        rid, pid = topo.addr(T.cores[qb], core)
+        g.remote_dma(B["ql"][:, 8 * t:8 * t + 8], B["qs"][:, 8 * t:8 * t + 8], T.sem["qa%d" % t], T.sem["qo%d" % t], pid, rid, topo.mask(core, T.cores[qb]))
+        lastw["ql%d" % t] = ("rem", ("qa%d" % t, len(topo.engines(T.cores[qf], core))))
+        for j in range(2):
+            ts("CG m%d" % j, "CGm", B["CGm"][:, 128 * j:128 * j + 128], B["CG"][:], sm("m%d" % j), None, A.mult)
+        cp("PB4u", "Ui", B["Ui"][:], U[:, 0:256])
+        ts("Ui", "U2", B["U2"][:], B["Ui"][:], 4095, None, A.bitwise_and)
+        tt("U2", "h1", B["h1"][:], B["U2"][:, 0:128], B["U2"][:, 128:256], A.mult)
+        ts("h1", "h2", B["h2"][:], B["h1"][:], 5, H - 1, A.logical_shift_right, A.bitwise_and)
+        tt("h2 U2", "hf", B["hf"][:], B["h2"][:], B["U2"][:, 128:256], A.add)
+        if t:
+            newcols(t - 1)
+
+        def ovcount(b):
+            mms("OV%d BD" % b, "PB6o", [(PB6[c32[b], k:128:16], B["OV"][:, 2 * b:2 * b + 2, k:256:16], bd8, True, True) for k in range(16)])
+
+        def eqmat(h):
+            for a in (2 * h, 2 * h + 1):
+                o = PD[h][:, 256 * (a % 2):256 * (a % 2) + 256]
+                mms("CG CGm NEG Id", "PD%d" % h, [(o, B["Id"][:], B["NEG"][:], True, False)])
+                if a % 2:
+                    wait("P", [("sP", cnt["P"] - 1)])
+                mms("CG CGm", "PD%d" % h, [(o, B["CG"][32 * a:32 * a + 32, :], B["CGm"][32 * a:32 * a + 32, :], False, True)])
+
+        def eqact(h):
+            act("PD%d" % h, "EQ%d" % h, B["EQ"][:, 512 * h:512 * h + 512], PD[h][:], F.Relu, bias=-10.0)
+        for n, b in enumerate(order):
+            act("PD%d" % b, "OV%d" % b, B["OV"][:, 2 * b:2 * b + 2, :], PD[b][:], F.Sign, bias=0.5)
+            if n == 1:
+                op("P", "hf IF", "PB4h", lambda: PE.transpose(U[:, 256:384], B["hf"][:], B["IF"][:, 0:128]))
+            ovcount(b)
+            if b == 0:
+                eqmat(0)
+        if t:
+            cp("PB4h", "H16", B["H16"][:], U[:, 256:384])
+        else:
+            cp("PB4h", "h1", B["h1"][:], U[:, 256:384])
+            ts("h1", "h2", B["h2"][:], B["h1"][:], H - 1, None, A.bitwise_and)
+            cp("h2", "H16", B["H16"][:], B["h2"][:])
+        bk = B["bk"][:] if t else B["bk"][:, 0:H]
+        BK = "bk0 bk1 bk2" if t else "bk0"
+        eqmat(1)
+        mms("Cf IF", "PB5", [(KS[:, 0:256], B["Cf"][:], B["IF"][:], True, False)])
+        for b in sb:
+            mms("one CK", "PB5", [(KS[c32[b], 0:256], B["one"][:, 0:32], B["CK"][:], False, False)])
+        def sbook(b):
+            act(BK + " H16", "BC%d" % b, B["BC"][:, ch[b]], bk.indirect(B["H16"][:, c32[b]]), F.Copy)
+
+        def vbook(b):
+            for c in (2 * b, 2 * b + 1):
+                tt(BK + " H16 D%d" % b, "IN%d" % b, B["IN"][:, c, :], bk.indirect(B["H16"][:, 16 * c:16 * c + 16]), B["D"][:, 256 * c:256 * c + 256], A.is_ge)
+
+        def bdiff(b):
+            mms("Id nId BC%d D%d" % (b, b), "PD%d" % b, [(PD[b][:], B["Id"][:], B["BC"][:, ch[b]], True, False), (PD[b][:], B["nId"][:], B["D"][:, ch[b]], False, True)])
+
+        def count(b):
+            mms("IN%d RB RBh" % b, "PB5", [(KS[c32[b], k:256:16], B["IN"][:, 2 * b:2 * b + 2, k:256:16], B["RBh" if b in sb else "RB"][:], False, False) for k in range(16)])
+        sbook(sb[0])
+        act(BK + " ql%d" % t, "ys%d" % t, B["ys"][:, L * t:L * t + L], bk.indirect(B["ql"][:, 8 * t:8 * t + 8]), F.Copy)
+        wait("G", deps("G", ["ys%d" % t], []))
+        rid, pid = topo.addr(T.cores[qf], core)
+        g.remote_dma(B["yl"][:, L * t:L * t + L], B["ys"][:, L * t:L * t + L], T.sem["ya%d" % t], T.sem["yo%d" % t], pid, rid, topo.mask(core, T.cores[qf]))
+        lastw["yl%d" % t] = ("rem", ("ya%d" % t, len(topo.engines(T.cores[qb], core))))
+        for b in sb[1:]:
+            sbook(b)
+        eqact(0)
+        vbook(vbk[0])
+        if t == 0:
+            late_consts()
+        op("V", ER + " lst", "evf", lambda: V.tensor_copy(B["evf"][:], B["E"][:, 128:128 + wg].indirect(v16)))
+        tt("evf Ci", "d4", B["d4"][:], B["evf"][:], B["Ci"][:], A.subtract)
+        tt("d4 P", "d4P", B["d4P"][:], B["d4"][:], B["P"][:], A.mult)
+        tt("fe P", "feP", B["feP"][:], B["fe"][:], B["P"][:], A.mult)
+        cp("OV0 OV1 OV2 OV3", "WO", B["WO"][:], B["OV"][:, :, 0:256:17])
+        mms("WO BD", "PB6o", [(PB6[:, 128:256], B["WO"][:], B["BD"][:], True, True)])
+        mms("d4 Iq fe Id d4P BDq feP BD16", "PB6k",
+            [(PB6[:, 256:384], B["d4"][:], B["Iq"][:], True, False), (PB6[:, 256:384], B["fe"][:], B["Id"][:], False, True),
+             (PB6[:, 384:512], B["d4P"][:], B["BDq"][:], True, False), (PB6[:, 384:512], B["feP"][:], B["BD16"][:], False, True)])
+        act("PB6o", "ov", B["ov"][:], PB6[:, 0:256], F.Relu, scale=-64.0, bias=128.0)
+        bdiff(sb[0])
+        count(vbk[0])
+        for b in vbk[1:]:
+            vbook(b)
+        for b in sb[1:]:
+            bdiff(b)
+        tt("PB6k ov", "Kc", B["Kc"][:], PB6[:, 256:512], B["ov"][:], A.add)
+        tt("evf Pb", "evP", B["evP"][:], B["evf"][:], B["Pb"][:], A.mult)
+        tt("P4 evP", "AAb", B["AA"][:, 128:256], B["P4"][:], B["evP"][:], A.subtract)
+        ts("Ci", "AAa", B["AA"][:, 0:128], B["Ci"][:], -4095.0, None, A.add)
+        tt("c128 e2", "BWa", B["BW"][:, 0:8], sm("c128"), vf, A.add)
+        if last:
+            cp("E E0 E1", "EF", B["EF"][:, 128:128 + M + L * t], B["E"][:, 128:128 + M + L * t])
+        for b in vbk[1:]:
+            count(b)
+        for b in sb:
+            act("PD%d" % b, "IN%d" % b, B["IN"][:, 2 * b:2 * b + 2, :], PD[b][:], F.Sign, bias=0.5)
+        count(sb[0])
+        for b in sb[1:]:
+            count(b)
+        mms("fe I14", "PB5", [(KS[:, 0:256], B["fe"][:], B["I14"][:], False, True)])
+        eqact(1)
+        for b in vbk:
+            cp("IN%d" % b, "WI", B["WI"][:, c32[b]], B["IN"][:, 2 * b:2 * b + 2, 0:256:17])
+        for b in sb:
+            ts("IN%d" % b, "WI", B["WI"][:, c32[b]], B["IN"][:, 2 * b:2 * b + 2, 0:256:17], 0.5, 0.5, A.mult, A.add)
+        mms("WI BD", "PB7s", [(PM[:, 384:512], B["WI"][:], B["BD"][:], True, True)])
+        tt("PB7s Kc", "wr", B["wr"][:], PM[:, 384:512], B["Kc"][:, 128:256], A.is_gt)
+        mms("nIh wr EQ0 EQ1", "PD0w", [(PD[0][:, 0:128], B["nIh"][:], B["wr"][:], True, False)]
+            + [(PD[0][:, 16 * k:16 * k + 16], B["EQ"][:, 128 * k:128 * k + 128], B["wr"][:, 16 * k:16 * k + 16], False, False) for k in range(8)]
+            + [(PD[0][:, 0:128], B["nIh"][:], B["wr"][:], False, True)])
+        sK = KS[:, 128:256]
+        tt("PB5 Kc", "cap", B["cap"][:], sK, B["Kc"][:, 0:128], A.is_gt)
+        tt("PB5 cap", "scap", B["scap"][:], sK, B["cap"][:], A.mult)
+        tt("PB5 Kc", "nc", B["nc"][:], sK, B["Kc"][:, 0:128], A.is_le)
+        op("V", "Mh scap", "scs", lambda: V.tensor_tensor_scan(B["scs"][:], B["Mh"][:], B["scap"][:], 0.0, A.mult, A.max))
+        for k in range(8):
+            ts("P scs", "sp", B["sp"][:, 16 * k:16 * k + 16], B["P"][:, 0:16], B["scs"][:, 16 * k + 15:16 * k + 16], None, A.mult)
+        tt("PB5 nc", "mk", B["mk"][:], KS[:, 0:128], B["nc"][:], A.mult)
+        tt("PD0w TPm", "wP", B["wP"][:], PD[0][:, 0:128], B["TPm"][:], A.is_lt)
+        op("V", "Mh mk", "sc", lambda: V.tensor_tensor_scan(B["sc"][:], B["Mh"][:], B["mk"][:], 0.0, A.mult, A.max))
+        for k in range(8):
+            ts("P sc", "zc", B["zc"][:, 16 * k:16 * k + 16], B["P"][:, 0:16], B["sc"][:, 16 * k + 15:16 * k + 16], None, A.mult)
+        tt("wr P", "wd", B["wd"][:], B["wr"][:], B["P"][:], A.mult)
+        mms("Id nId x yl%d" % t, "PB4d", [(U[:, 256:384], B["Id"][:], x, True, False), (U[:, 256:384], B["nId"][:], B["yl"][:, L * t:L * t + L], False, True)])
+        act("PB4d", "nx", nx, U[:, 256:384], F.Abs)
+        act("PD0w", "wL", B["wL"][:], PD[0][:, 0:128], F.Relu, scale=-1.0)
+        mms("IF evP Pn P128 Id", "PB6v", [(PB6[:, 0:128], B["IF"][:, 0:128], B["evP"][:], True, False), (PB6[:, 0:128], B["IF"][:, 0:128], B["Pn"][:], False, False)]
+            + [(PB6[:, 0:128], B["Id"][:], B["P128"][:], False, False)] * t)
+        mms("cap Id", "PD3c", [(PD[3][:, 0:128], B["cap"][:], B["Id"][:], True, True)])
+        mms("sp I4", "PB6v", [(PB6[:, 0:128], B["sp"][:], B["I4"][:], False, True)])
+        mms("LW nx", "PB4b", [(U[:, 384:392], B["LW"][:, 128 * r:128 * r + 128], B["XX"][:, r:128:16], r == 0, r == 15) for r in range(16)])
+        cp("PB4b", "bk1", sm("bk1"), U[:, 384:392])
+        ts("bk1", "bk2", sm("bk2"), sm("bk1"), R - 1, None, A.bitwise_and)
+        tt("bk2 e2", "BWb", B["BW"][:, 8:16], sm("bk2"), vf, A.subtract)
+        mms("Id nx x one CA", "PB4a", [(U[:, 0:256], B["Id"][:], B["XX"][:], True, False), (U[:, 0:256], B["one"][:], B["CA"][:], False, False)])
+        mms("wP CH2", "PD2l", [(PD[2][:, 0:16], B["wP"][:], B["CH2"][:], True, True)])
+        mms("zc BDf", "PD2l", [(PD[2][:, 24:32], B["zc"][:], B["BDf"][:], True, True)])
+        mms("wd CH2", "PD2l", [(PD[2][:, 16:24], B["wd"][:], B["CH2"][:, 0:8], True, True)])
+        mms("wL JJ", "PB4a", [(U[:, 0:256], B["wL"][:], B["JJ"][:], False, True)])
+        mms("x Id one CA wL JJ", "PD1x", [(PD[1][:, 0:128], B["Id"][:], x, True, False), (PD[1][:, 0:128], B["one"][:], B["CA"][:, 0:128], False, False),
+                                          (PD[1][:, 0:128], B["wL"][:], B["JJ"][:, 0:128], False, True)])
+        mms("cap scap wL Id I4", "PB5n", [(KS[:, 0:128], B["cap"][:], B["Id"][:], True, True), (KS[:, 128:256], B["scap"][:], B["I4"][:], True, True),
+                                          (KS[:, 256:384], B["wL"][:], B["Id"][:], True, True)])
+        act("PB4a", "xm", B["xm"][:], U[:, 0:256], F.Relu)
+        act("PD1x", "X", B["X"][:, M + L * t:M + L * t + L], PD[1][:, 0:128], F.Relu)
+        if not last:
+            mms("xm Id", "PB7x", [(PM[:, 256:384], B["xm"][:, 0:128], B["Id"][:], True, False), (PM[:, 256:384], B["xm"][:, 128:256], B["Id"][:], False, True)])
+        mms("xm Id", "PB4x", [(U[:, 256:384], B["Id"][:], B["xm"][:, 0:128], True, False), (U[:, 256:384], B["Id"][:], B["xm"][:, 128:256], False, True)])
+        if not last:
+            act("PB7x", "xT", B["xT"][:], PM[:, 256:384], F.Copy)
+        act("PB4x", "x", x, U[:, 256:384], F.Copy)
+        tt("PD3c AAb", "mmb", B["mm"][:, 128:256], PD[3][:, 0:128], B["AA"][:, 128:256], A.mult)
+        cp("PD2l", "ch1", sm("ch1"), PD[2][:, 24:32])
+        ts("ch1", "ch2", sm("ch2"), sm("ch1"), 2047, None, A.bitwise_and)
+        tt("e2 ch2", "ch3", sm("ch3"), vf, sm("ch2"), A.subtract)
+        tt("PD2l ch3", "ch4", sm("ch4"), PD[2][:, 16:24], sm("ch3"), A.mult)
+        tt("ch2 ch4", "BBb", B["BB"][:, 8:16], sm("ch2"), sm("ch4"), A.add)
+        tt("PD2l BWa BWb", "e1", sm("e1"), PD[2][:, 0:16], B["BW"][:], A.mult)
+        tt("e1 BBa BBb", "e2", B["e2"][:], sm("e1"), B["BB"][:], A.add)
+        cp("e2", "lst", B["lst"][:], B["e2"][:])
+        tt("PB6v mmb", "VC", B["VC"][:], PB6[:, 0:128], B["mm"][:, 128:256], A.add)
+        if not last:
+            op("V", "lst VC", ER, lambda: V.tensor_copy(B["E"][:, 0:128 + wg].indirect(B["lst"][:, 0:8]), B["VC"][:]))
+        else:
+            op("V", "lst VC EF", "EF", lambda: V.tensor_copy(B["EF"][:, 0:128 + wg].indirect(B["lst"][:, 0:8]), B["VC"][:]))
+            dma("Y", "EF", "", "out", T.ykids[:, 0:M + L * t], B["EF"][:, 128:128 + M + L * t])
+            newcols(t)
+            dma("Y", "EF%d" % t, "", "out", T.ykids[:, M + L * t:M + L * t + L], B["EF"][:, 128 + M + L * t:128 + M + L * t + L])
+            dma("S", "X", "", "out", T.ynodes[:], B["X"][:, M:M + L * STEPS])
+            dma("S", "x", "", "out", T.ycand[:], x)
+            dma("S", "e2", "", "out", T.yspot[:], vf)
+    for t in range(STEPS):
+        for s in ("qo", "yo"):
+            g.wait_ge(T.sem[s + str(t)], neng)
+    g.wait_ge(T.sem.wloc, neng * (NB - 1))
+    wait("G", [("sV", cnt["V"]), ("sS", cnt["S"]), ("sP", cnt["P"]), ("sG", cnt["G"])] + [("d_" + k, n) for k, n in dcount.items()]
+         + [("wrem", neng * (NB - 1))] + [(k + str(t), neng) for k in ("qa", "ya") for t in range(STEPS)])

@@ -1,9 +1,10 @@
+import numpy as np
 from concourse.mybir import AluOpType as A, ActivationFunctionType as F
 
 M, L, STEPS, H, R, NB = 896, 128, 3, 2048, 512, 4
 XW = 1296
 SBANKS = (2, 3)
-XS = (3,)
+XS = (1, 2)
 
 BF, F32, I32, U16 = "bfloat16", "float32", "int32", "uint16"
 _S = {
@@ -13,7 +14,7 @@ _S = {
     "one": (128, BF), "zer": (256, BF), "pk": (128, I32), "Id": (128, BF), "nId": (128, BF), "IF": (256, F32), "JJ": (256, BF), "CA": (256, BF),
     "BD0": (128, BF), "BD": (128, BF), "BDf": (8, F32), "P": (128, BF), "Pb": (128, BF), "P4": (128, F32), "P128": (128, BF), "TPm": (128, BF),
     "NEG": (256, BF), "I4": (128, BF), "Iq": (128, BF), "I14": (256, BF), "nIh": (128, BF), "BDq": (128, BF), "BD16": (128, BF), "CH2": (16, BF),
-    "RB": (16, BF), "RBh": (16, BF), "WO": (128, BF), "WI": (128, BF), "CK": (256, BF), "Ex": (2048, BF), "Mh": (128, BF), "W": (16, BF), "Wz": (48, BF),
+    "RB": (16, BF), "WO": (128, BF), "WI": (128, BF), "Ex": (2048, BF), "Mh": (128, BF), "W": (16, BF), "Wz": (48, BF),
     "LW": (2048, BF), "lwo": (2, U16), "wrep": (16, BF), "chp": (8, BF),
     "ni": (128, F32), "Pn": (128, F32), "pt": (128, I32), "ptb": (256, BF), "lowb": (128, BF), "hib": (16, F32), "CODE": (1280, BF),
     "lst": (16, U16), "e2": (16, F32), "BW": (16, F32), "BB": (16, F32),
@@ -34,9 +35,20 @@ for _k in ("PD0", "PD1", "PD2", "PD3", "PB4", "PB5", "PB6", "PB7"):
 _I8 = {"uz": (0, 16), "uz2": (16, 16), "hz1": (32, 8), "hz2": (40, 8), "bk1": (48, 8), "bk2": (56, 8), "ch1": (64, 8), "ch2": (72, 8),
        "ip": (80, 1), "p15": (84, 1), "mi": (88, 1), "g8": (96, 8)}
 _F8 = {"hz": (0, 8), "ch3": (8, 8), "ch4": (16, 8), "il": (24, 8), "c128": (32, 8), "e1": (40, 16), "lwi": (56, 1), "colk": (60, 1), "m0": (64, 1),
-       "m1": (68, 1), "lwf": (72, 1)}
-SLICED = set("Ex W JJ I14 CH2 RB RBh CK CA ptb zh zc sp IF WI CGm Wz CODE IN0 IN1 IN2 IN3".split())
-DMAS = ["spi", "E", "x", "X", "wt", "bk0", "bk1", "bk2", "out"]
+       "m1": (68, 1), "lwf": (72, 1), "cb": (76, 1)}
+SLICED = set("pt Ex W JJ I14 CH2 RB RBh CK CA ptb zh zc sp IF WI CGm Wz CODE IN0 IN1 IN2 IN3 PB7".split())
+DUR = {"V": 0.13, "S": 0.19, "P": 0.13, "G": 0.4, "Y": 0.1, "A": 0.0}
+COST = {"VCi": 0.24, "VXC": 0.82, "Vevf": 0.24, "VXV": 0.24, "VE": 0.43, "VEF": 0.43, "VUi": 0.26, "VU": 0.26, "Vh": 0.26, "Vhf": 0.26, "VIN": 0.47,
+        "Vd": 0.26, "VKc": 0.26, "VLW": 0.1, "SD": 0.57, "SOV": 0.57, "SEQ": 0.57, "SXC": 0.82, "SBC": 0.82, "Sov": 0.32, "Sxm": 0.32, "SCG": 0.25,
+        "Sys": 0.25, "PPD": 0.26, "PPDw": 0.38, "PPB": 0.4, "PPBu": 0.5, "PPBh": 0.26, "PPBo": 0.3, "PPBk": 0.26, "PPBv": 0.3, "PPDb": 0.52}
+for _k in ("uz", "uz2", "hz1", "hz2", "hz", "zh", "qs", "zc", "sp", "ch1", "ch2", "ch3", "ch4", "BBb", "BWa", "BWb", "bk1", "bk2", "e1", "e2", "lst", "WI", "WO",
+           "CODE", "Ex", "W", "Wz", "RB", "CH2", "nId", "pt", "ptb", "CGm", "lwi", "lwf", "lwo", "il", "c128", "BBa", "BDf", "p15", "colk", "m0", "m1", "mi",
+           "chp", "wrep", "Pb"):
+    COST["V" + _k.rstrip("0123456789")] = 0.065
+COST["Sspk"] = COST["Spsk"] = 0.13
+TUNE = {"wake": 0.13, "remote": 2.5, "look": 0.02, "noise": 0.1, "seed": 9594}
+ORDERS = {}
+DMAS = ["spi", "E", "x", "X", "wt", "bk0", "bk1", "bk2", "out", "out0"]
 SEMAPHORES = (["sV", "sS", "sP", "sG", "wloc", "wrem"] + ["d_" + k for k in DMAS]
               + [k + str(t) for k in ("qa", "qo", "ya", "yo") for t in range(STEPS)])
 
@@ -69,57 +81,61 @@ def rank_program(g, core, T, topo):
             for a, b in snap.get((s, v), {}).items():
                 known[eng][a] = max(known[eng].get(a, 0), b)
 
-    def deps(eng, rd, wr):
-        toks = []
-        for k in rd:
-            if k in lastw:
-                toks.append(lastw[k][1])
-        for k in wr:
-            if k in lastw and (lastw[k][0] != eng or (eng != "P" and k not in SLICED)):
-                toks.append(lastw[k][1])
-            for e, t in readers.get(k, {}).items():
-                if e != eng or eng != "P":
-                    toks.append(t)
-        for k in list(rd) + list(wr):
-            if k[:2] in ("PD", "PB"):
-                for e, t in banks.get(k[:3], {}).items():
-                    if e != eng:
-                        toks.append(t)
-        return toks
+    calls = []
 
-    def done(eng, tok, rd, wr):
-        snap[tok] = dict(known[eng])
-        for k in wr:
-            lastw[k] = (eng, tok)
-            readers[k] = {}
-        for k in rd:
-            readers.setdefault(k, {})[eng] = tok
-        for k in list(rd) + list(wr):
-            if k[:2] in ("PD", "PB"):
-                banks.setdefault(k[:3], {})[eng] = tok
-
-    def op(eng, rd, wr, fn):
+    def note(eng, rd, wr, fn, kind="c", dur=None, lat=0.0, tok=None):
         rd, wr = rd.split(), wr.split()
-        wait(eng, deps(eng, rd, wr))
-        i = fn()
-        cnt[eng] += 1
-        i.then_inc(T.sem["s" + eng], 1)
-        done(eng, ("s" + eng, cnt[eng]), rd, wr)
+        n, pre = len(calls), {}
+
+        def edge(m, w):
+            pre[m] = pre.get(m, False) or w
+        for k in rd:
+            for m in lastw.get(k, ()):
+                edge(m, True)
+        for k in wr:
+            old, rs = lastw.get(k, []), readers.get(k, [])
+            if k in SLICED and old and not rs and calls[old[0]]["eng"] == eng:
+                lastw[k] = old + [n]
+                for m in calls[old[0]]["pre"]:
+                    if calls[old[0]]["pre"][m]:
+                        edge(m, True)
+                continue
+            for m in old:
+                edge(m, not (eng == "P" and calls[m]["eng"] == "P"))
+            for m in rs:
+                edge(m, not (eng == "P" and calls[m]["eng"] == "P"))
+            lastw[k], readers[k] = [n], []
+        for k in rd:
+            readers.setdefault(k, []).append(n)
+        for k in sorted(set(k[:3] for k in rd + wr if k[:2] in ("PD", "PB"))):
+            cur, prev = banks.get(k, (None, [])), None
+            if cur[0] != eng:
+                banks[k] = cur = (eng, [], cur[1])
+            for m in cur[2]:
+                edge(m, True)
+            if eng == "P":
+                for m in cur[1]:
+                    edge(m, False)
+            cur[1].append(n)
+        calls.append({"eng": eng, "pre": pre, "fn": fn, "kind": kind, "lat": lat, "tok": tok, "n": n,
+                      "dur": dur if dur is not None else COST.get(eng + wr[0].rstrip("0123456789"), DUR[eng])})
+        return n
+
+    def op(eng, rd, wr, fn, dur=None):
+        return note(eng, rd, wr, fn, dur=dur)
 
     dcount = {}
 
-    def dma(eng, rd, wr, sem, out, in_):
-        rd, wr = rd.split(), wr.split()
-        wait(eng, deps(eng, rd, wr))
-        Q[eng].dma_start(out, in_).then_inc(T.sem["d_" + sem], 16)
+    def dma(eng, rd, wr, sem, out, in_, lat=3.0):
         dcount[sem] = dcount.get(sem, 0) + 16
-        tok = ("d_" + sem, dcount[sem])
-        snap[tok] = dict(known[eng])
-        for k in wr:
-            lastw[k] = ("dma", tok)
-            readers[k] = {}
-        for k in rd:
-            readers.setdefault(k, {})["dma" + sem] = tok
+        note(eng, rd, wr, lambda: Q[eng].dma_start(out, in_).then_inc(T.sem["d_" + sem], 16), "d", 0.1, lat, ("d_" + sem, dcount[sem]))
+
+    def send(rd, wr, out, in_, dst, arrive, left, lands):
+        rid, pid = topo.addr(dst, core)
+        m = note("G", rd, "", lambda: g.remote_dma(out, in_, T.sem[arrive], T.sem[left], pid, rid, topo.mask(core, dst)), "r", 0.4)
+        if wr:
+            n = note("A", "", wr, None, "a", 0.0, TUNE["remote"], (arrive, lands))
+            calls[n]["pre"][m] = True
 
     V, S, PE = g.vector, g.scalar, g.tensor
 
@@ -166,33 +182,25 @@ def rank_program(g, core, T, topo):
     op("G", "", "pk", lambda: g.iota(B["pk"][:], [[0, 8], [-1, 16]], 16, 1))
     op("G", "", "ip", lambda: g.iota(sm("ip"), [[0, 1]], 0, 1))
     op("G", "", "g8", lambda: g.iota(sm("g8"), [[0, 8]], 0, 1))
-    wait("G", deps("G", ["wt"], []))
-    for j in range(NB - 1):
-        d = T.cores[(rank - 1 - j) % NB]
-        rid, pid = topo.addr(d, core)
-        g.remote_dma(B["wl%d" % j][:], B["wt"][:], T.sem.wrem, T.sem.wloc, pid, rid, topo.mask(core, d))
     neng = len(topo.engines(core, T.cores[(rank + 1) % NB]))
     for j in range(NB - 1):
-        lastw["wl%d" % j] = ("rem", ("wrem", neng * (NB - 1)))
+        send("wt", "wl0 wl1 wl2" if j == NB - 2 else "", B["wl%d" % j][:], B["wt"][:], T.cores[(rank - 1 - j) % NB], "wrem", "wloc", neng * (NB - 1))
     op("G", "zer", "NEG", lambda: g.affine_select(B["NEG"][:], B["zer"][:], [[0, 2], [1, 128]], A.is_gt, -100.0, 0, -1))
     op("G", "", "ni", lambda: g.iota(B["ni"][:], [[1, 128]], M, 0, allow_small_or_imprecise_dtypes=True))
     op("G", "", "LW", lambda: g.iota(B["LW"][:], [[0, 2048]], 0, 0, allow_small_or_imprecise_dtypes=True))
 
-    cp("spi", "lst", B["lst"][:, 8:16], B["spi"][:])
-    cp("spi", "e2", B["e2"][:, 8:16], B["spi"][:])
     memset("Xz", B["X"][:, M:XW], 0.0)
-    memset("ptb0", B["ptb"][:], 0.0)
+    memset("ptb0", B["ptb"][:, 128:256], 0.0)
+    memset("pt0", B["pt"][:], 0)
     memset("Mh", B["Mh"][:], 1.0)
     memset("Mh", B["Mh"][:, 0:128:16], 0.0)
     memset("IF", B["IF"][:, 128:256], 0.0)
     memset("CA", B["CA"][:, 0:128], -2.0)
     memset("CA", B["CA"][:, 128:256], 0.0)
-    for j in range(2):
-        memset("CK", B["CK"][:, 128 * j:128 * j + 128], (2048.0, 0.0625)[j])
     bd8 = B["BD"][:, 0:128:16]
     ts("Id", "nId", B["nId"][:], B["Id"][:], -1.0, None, A.mult)
-    mms("x Id", "PB7x", [(B["PB7"][:, 256:384], x, B["Id"][:], True, True)])
-    act("PB7x", "xT", B["xT"][:], B["PB7"][:, 256:384], F.Copy)
+    mms("x Id", "PB4x", [(B["PB4"][:, 384:512], x, B["Id"][:], True, True)])
+    act("PB4x", "xT", B["xT"][:], B["PB4"][:, 384:512], F.Copy)
     EXR = "Ex"
     for k in range(16):
         if k % 3 == 2:
@@ -200,8 +208,6 @@ def rank_program(g, core, T, topo):
             EXR += " Ex%d" % k
         else:
             cp("Id", "Ex", B["Ex"][:, k:2048:16], B["Id"][:])
-    for u in range(2):
-        ts("BD wt", "W", B["W"][:, 8 * u:8 * u + 8], bd8, B["wt"][:, u:u + 1], None, A.mult)
     ts("pk", "Ci", B["Ci"][:], B["pk"][:], 15, None, A.bitwise_and)
     ts("Ci", "P", B["P"][:], B["Ci"][:], 0, None, A.is_equal)
     cp("Id", "IF", B["IF"][:, 0:128], B["Id"][:])
@@ -209,39 +215,48 @@ def rank_program(g, core, T, topo):
     ts("ip", "p15", sm("p15"), sm("ip"), 15, None, A.bitwise_and)
     ts("p15", "colk", sm("colk"), sm("p15"), -2048.0, 30720.0, A.mult, A.add)
     ts("P", "Pb", B["Pb"][:], B["P"][:], -1.0, 1.0, A.mult, A.add)
-    ts("P", "TPm", B["TPm"][:], B["P"][:], 1000.0, -1000.0, A.mult, A.add)
-    ts("Pb", "P4", B["P4"][:], B["Pb"][:], 4095.0, None, A.mult)
-    for k, src, f in (("P128", "P", 128.0), ("I4", "Id", 4096.0), ("Iq", "Id", 1.0 / 4096), ("nIh", "Id", -0.5), ("BDq", "BD", 1.0 / 4096),
+    CP, CPb, CP4 = (B["PB7"][:, 128 * j:128 * j + 128] for j in range(3))
+    cp("P", "PB7", CP, B["P"][:])
+    cp("Pb", "PB7", CPb, B["Pb"][:])
+    ts("Pb", "PB7", CP4, B["Pb"][:], 4095.0, None, A.mult)
+    act("P", "TPm", B["TPm"][:], B["P"][:], F.Copy, scale=1000.0, bias=-1000.0)
+    act("colk", "cb", sm("cb"), sm("colk"), F.Copy, scale=-1.0, bias=-4095.0)
+    for k, src, f in (("nIh", "Id", -0.5), ("I4", "Id", 4096.0), ("Iq", "Id", 1.0 / 4096), ("P128", "P", 128.0), ("BDq", "BD", 1.0 / 4096),
                       ("BD16", "BD", -16.0)):
-        ts(src, k, B[k][:], B[src][:], f, None, A.mult)
+        act(src, k, B[k][:], B[src][:], F.Copy, scale=f)
+    memset("I14z", B["I14"][:, 128:256], 0.0)
+    act("Id", "I14", B["I14"][:, 0:128], B["Id"][:], F.Copy, scale=-16384.0)
     for j in range(2):
-        ts("Id", "I14", B["I14"][:, 128 * j:128 * j + 128], B["Id"][:], (-16384.0, 0.0)[j], None, A.mult)
-        ts("Id", "JJ", B["JJ"][:, 128 * j:128 * j + 128], B["Id"][:], (256.0, -256.0)[j], None, A.mult)
+        act("Id", "JJ", B["JJ"][:, 128 * j:128 * j + 128], B["Id"][:], F.Copy, scale=(256.0, -256.0)[j])
         cp("BD", "CH2", B["CH2"][:, 8 * j:8 * j + 8], bd8)
         ts("BD", "RB", B["RB"][:, 8 * j:8 * j + 8], bd8, (32768.0, 1.0)[j], None, A.mult)
-        ts("BD", "RBh", B["RBh"][:, 8 * j:8 * j + 8], bd8, (16384.0, 0.5)[j], None, A.mult)
     pt = B["pt"]
     for b in range(7):
-        ts("g8", "pt%d" % b, pt[:, b:128:16], sm("g8"), b, 1, A.logical_shift_right, A.bitwise_and)
-    for b in range(7):
-        ts("ptb0 pt%d" % b, "ptb", B["ptb"][:, b:128:16], pt[:, b:128:16], 2.0, -1.0, A.mult, A.add)
+        ts("g8 pt0", "pt", pt[:, b:128:16], sm("g8"), b, 1, A.logical_shift_right, A.bitwise_and)
+    ts("pt", "ptb", B["ptb"][:, 0:128], pt[:], 2.0, -1.0, A.mult, A.add)
     for b in range(7, 11):
-        ts("pt%d" % (b - 7), "ptb", B["ptb"][:, 128 + b:256:16], pt[:, b - 7:128:16], 2.0, -1.0, A.mult, A.add)
-    mms("ptb Id", "PB7c", [(B["PB7"][:, 256:384], B["ptb"][:, 0:128], B["Id"][:], True, True),
-                           (B["PB7"][:, 384:400], B["ptb"][:, 128:256], B["Id"][:, 0:16], True, True)])
-    act("PB7c", "hib", B["hib"][:], B["PB7"][:, 384:400], F.Copy)
-    act("PB7c", "lowb", B["lowb"][:], B["PB7"][:, 256:384], F.Copy)
-    for h in range(10):
-        act("lowb hib", "CODE", B["CODE"][:, 128 * h:128 * h + 128], B["lowb"][:], F.Identity, bias=B["hib"][:, h:h + 1])
+        ts("ptb0 pt", "ptb", B["ptb"][:, 128 + b:256:16], pt[:, b - 7:128:16], 2.0, None, A.mult)
+    mms("ptb Id", "PB6c", [(B["PB6"][:, 256:384], B["ptb"][:, 0:128], B["Id"][:], True, True),
+                           (B["PB6"][:, 384:400], B["ptb"][:, 128:256], B["Id"][:, 0:16], True, True)])
+    act("PB6c", "hib", B["hib"][:], B["PB6"][:, 384:400], F.Copy)
+    act("PB6c", "lowb", B["lowb"][:], B["PB6"][:, 256:384], F.Copy)
     ts("ip", "mi", sm("mi"), sm("ip"), 4, 1, A.logical_shift_right, A.bitwise_and)
     cp("mi", "m1", sm("m1"), sm("mi"))
     ts("m1", "m0", sm("m0"), sm("m1"), -1.0, 1.0, A.mult, A.add)
     cp("ip", "lwi", sm("lwi"), sm("ip"))
     ts("BD lwi", "chp", B["chp"][:], bd8, sm("lwi"), None, A.mult)
-    mms("P chp", "PB7i", [(B["PB7"][:, 152:160], B["P"][:], B["chp"][:], True, True)])
-    cp("PB7i", "il", sm("il"), B["PB7"][:, 152:160])
+    mms("P chp", "PD3i", [(B["PD3"][:, 0:8], B["P"][:], B["chp"][:], True, True)])
+    cp("PD3i", "il", sm("il"), B["PD3"][:, 0:8])
     ts("il", "c128", sm("c128"), sm("il"), -1.0, 128.0, A.mult, A.add)
     cp("il", "BBa", B["BB"][:, 0:8], sm("il"))
+    for u in range(2):
+        ts("BD wt", "W", B["W"][:, 8 * u:8 * u + 8], bd8, B["wt"][:, u:u + 1], None, A.mult)
+    cp("spi", "lst", B["lst"][:, 8:16], B["spi"][:])
+    cp("spi", "e2", B["e2"][:, 8:16], B["spi"][:])
+
+    def code_blocks():
+        for h in range(10):
+            ts("lowb hib", "CODE", B["CODE"][:, 128 * h:128 * h + 128], B["lowb"][:], B["hib"][:, h:h + 1], None, A.add)
 
     def late_consts():
         tt("P ni", "Pn", B["Pn"][:], B["P"][:], B["ni"][:], A.mult)
@@ -251,12 +266,13 @@ def rank_program(g, core, T, topo):
         op("V", "lwo wrep LW", "LW", lambda: V.tensor_copy(B["LW"][:].indirect(B["lwo"][:, 0:1]), B["wrep"][:]))
 
     PD = [B["PD%d" % b] for b in range(4)]
-    U, KS, PB6, PM = B["PB4"], B["PB5"], B["PB6"], B["PB7"]
+    U, KS, PB6 = B["PB4"], B["PB5"], B["PB6"]
     v16, vf = B["lst"][:, 8:16], B["e2"][:, 8:16]
     sb = list(SBANKS)
     vbk = [b for b in range(4) if b not in sb]
     vb = [b for b in range(4) if b not in XS]
-    order = vb[:1] + list(XS) + vb[1:]
+    order = list(range(4))
+    dorder = list(XS) + vb
     ch = [slice(512 * b, 512 * b + 512) for b in range(4)]
     c32 = [slice(32 * b, 32 * b + 32) for b in range(4)]
 
@@ -268,46 +284,55 @@ def rank_program(g, core, T, topo):
         c = 128 + M + L * t
         ts("n2", k + str(t), B[k][:, c:c + L], B["n2"][:], 4095.0, None, A.add)
 
+    def nodes_at(t):
+        op("V", "X lst " + " ".join("X%d" % j for j in range(t - 1)), "XV",
+           lambda: V.tensor_copy(B["XV"][:], B["X"][:, 0:M + L * max(0, t - 1)].indirect(v16)))
+
+    def newx():
+        mms("xm Id", "PB4x", [(U[:, 256:384], B["Id"][:], B["xm"][:, 0:128], True, False), (U[:, 256:384], B["Id"][:], B["xm"][:, 128:256], False, True)])
+        act("PB4x", "x", x, U[:, 256:384], F.Copy)
+
     for t in range(STEPS):
         last = t == STEPS - 1
         wg = M + L * max(0, t - 1)
+        XR = "X Xz " + " ".join("X%d" % j for j in range(t))
         ER = "E " + " ".join("E%d" % j for j in range(t - 1))
         qb = (rank + 1 + t) % NB
         qf = (rank - 1 - t) % NB
         ts(ER + " lst", "Ci", B["Ci"][:], B["E"][:, 128:128 + wg].indirect(v16), 4095, None, A.bitwise_and)
         ts("Ci", "C16", B["C16"][:], B["Ci"][:], 1280.0, None, A.min)
-        act("X Xz lst", "XV", B["XV"][:], B["X"][:].indirect(v16), F.Copy)
+        if t == 0:
+            nodes_at(t)
+        mms("XV xm Id nId x", "PB5z", [(KS[:, 384:512], B["Id"][:], B["XV"][:], True, False)]
+            + ([(KS[:, 384:512], B["nId"][:], x, False, True)] if t == 0 else
+               [(KS[:, 384:512], B["nId"][:], B["xm"][:, L * j:L * j + L], False, j == 1) for j in range(2)]))
+        act("PB5z", "z", B["z"][:], KS[:, 384:512], F.Abs)
+        if t:
+            mms("z Wz", "PB5u", [(KS[:, 384:400], B["z"][:], B["Wz"][:, 16 * t:16 * t + 16], True, True)])
         for b in order:
             mms("%s xT" % EXR, "PD%d" % b, [(PD[b][:], B["xT"][:], B["Ex"][:, ch[b]], True, False)])
 
         def diff(b):
             mms("nId XC%d" % b, "PD%d" % b, [(PD[b][:], B["nId"][:], B["XC"][:, ch[b]], False, True)])
 
-        def hashsum(b):
-            mms("D%d W" % b, "PB4u", [(U[c32[b], k:256:16], B["D"][:, 512 * b + k:512 * b + 512:16], B["W"][:], True, True) for k in range(16)])
+        def hashsum(b0, b1):
+            mms(" ".join("D%d" % b for b in range(b0, b1)) + " W", "PB4u",
+                [(U[32 * b0:32 * b1, k:256:16], B["D"][:, 512 * b0 + k:512 * b1:16], B["W"][:], True, True) for k in range(16)])
 
         for b in XS:
-            act("X Xz C16", "XC%d" % b, B["XC"][:, ch[b]], B["X"][:].indirect(B["C16"][:, c32[b]]), F.Copy)
-        mms("XV x Id nId", "PB7z", [(PM[:, 0:128], B["Id"][:], B["XV"][:], True, False), (PM[:, 0:128], B["nId"][:], x, False, True)])
-        act("PB7z", "z", B["z"][:], PM[:, 0:128], F.Abs)
+            act(XR + " C16", "XC%d" % b, B["XC"][:, ch[b]], B["X"][:].indirect(B["C16"][:, c32[b]]), F.Copy)
+        if t:
+            newx()
         if t == 0:
+            for b in vb[:-1]:
+                cp(XR + " C16", "XC%d" % b, B["XC"][:, ch[b]], B["X"][:].indirect(B["C16"][:, c32[b]]))
+            for b in dorder[:-1]:
+                diff(b)
             for j in range(3):
                 for u in range(2):
                     ts("BD wl%d" % j, "Wz", B["Wz"][:, 16 * j + 8 * u:16 * j + 8 * u + 8], bd8, B["wl%d" % j][:, u:u + 1], None, A.mult)
-        for b in vb:
-            cp("X Xz C16", "XC%d" % b, B["XC"][:, ch[b]], B["X"][:].indirect(B["C16"][:, c32[b]]))
-        diff(order[0])
-        mms("z Wz", "PB7u", [(PM[:, 128:144], B["z"][:], B["Wz"][:, 16 * t:16 * t + 16], True, True)])
-        for b in order[1:3]:
-            diff(b)
-        act("CODE lst", "CG", B["CG"][:], B["CODE"][:].indirect(v16), F.Copy)
-        for n, b in enumerate(order):
-            if n == 1:
-                diff(order[3])
-            act("PD%d" % b, "D%d" % b, B["D"][:, ch[b]], PD[b][:], F.Abs)
-            if n < 3:
-                hashsum(b)
-        cp("PB7u", "uz", sm("uz"), PM[:, 128:144])
+            mms("z Wz", "PB5u", [(KS[:, 384:400], B["z"][:], B["Wz"][:, 16 * t:16 * t + 16], True, True)])
+        cp("PB5u", "uz", sm("uz"), KS[:, 384:400])
         ts("uz", "uz2", sm("uz2"), sm("uz"), 4095, None, A.bitwise_and)
         tt("uz2", "hz1", sm("hz1"), sm("uz2", 0, 8), sm("uz2", 8, 16), A.mult)
         ts("hz1", "hz2", sm("hz2"), sm("hz1"), 5, H - 1, A.logical_shift_right, A.bitwise_and)
@@ -319,15 +344,35 @@ def rank_program(g, core, T, topo):
             cp("hz2", "hz", sm("hz"), sm("hz2"))
         for k in range(8):
             ts("P hz", "zh", B["zh"][:, 16 * k:16 * k + 16], B["P"][:, 0:16], sm("hz", k, k + 1), None, A.mult)
-        mms("zh BDf", "PB7q", [(PM[:, 144:152], B["zh"][:], B["BDf"][:], True, True)])
-        hashsum(order[3])
+        mms("zh BDf", "PB5q", [(KS[:, 400:408], B["zh"][:], B["BDf"][:], True, True)])
+        if t:
+            for b in XS:
+                diff(b)
         ts("Ci", "fe", B["fe"][:], B["Ci"][:], 4095.0, 128.0, A.is_ge, A.mult)
         ts("Ci colk", "Cf", B["Cf"][:], B["Ci"][:], sm("colk"), None, A.add)
-        cp("PB7q", "qs%d" % t, B["qs"][:, 8 * t:8 * t + 8], PM[:, 144:152])
-        wait("G", deps("G", ["qs%d" % t], []))
-        rid, pid = topo.addr(T.cores[qb], core)
-        g.remote_dma(B["ql"][:, 8 * t:8 * t + 8], B["qs"][:, 8 * t:8 * t + 8], T.sem["qa%d" % t], T.sem["qo%d" % t], pid, rid, topo.mask(core, T.cores[qb]))
-        lastw["ql%d" % t] = ("rem", ("qa%d" % t, len(topo.engines(T.cores[qf], core))))
+        cp("PB5q", "qs%d" % t, B["qs"][:, 8 * t:8 * t + 8], KS[:, 400:408])
+        send("qs%d" % t, "ql%d" % t, B["ql"][:, 8 * t:8 * t + 8], B["qs"][:, 8 * t:8 * t + 8], T.cores[qb], "qa%d" % t, "qo%d" % t,
+             len(topo.engines(T.cores[qf], core)))
+        for b in vb if t else vb[-1:]:
+            cp(XR + " C16", "XC%d" % b, B["XC"][:, ch[b]], B["X"][:].indirect(B["C16"][:, c32[b]]))
+            if b != 3:
+                diff(b)
+        for n, b in enumerate(dorder):
+            act("PD%d" % b, "D%d" % b, B["D"][:, ch[b]], PD[b][:], F.Abs)
+            if n == 0 and t:
+                act("CODE lst", "CG", B["CG"][:], B["CODE"][:].indirect(v16), F.Copy)
+            if n == 1:
+                diff(3)
+            if n == 2:
+                hashsum(0, 3)
+        hashsum(3, 4)
+        if t == 0:
+            code_blocks()
+            act("CODE lst", "CG", B["CG"][:], B["CODE"][:].indirect(v16), F.Copy)
+        op("V", ER + " lst", "evf", lambda wg=wg: V.tensor_copy(B["evf"][:], B["E"][:, 128:128 + wg].indirect(v16)))
+        tt("evf Ci", "d4", B["d4"][:], B["evf"][:], B["Ci"][:], A.subtract)
+        tt("d4 PB7", "d4P", B["d4P"][:], B["d4"][:], CP, A.mult)
+        tt("fe PB7", "feP", B["feP"][:], B["fe"][:], CP, A.mult)
         for j in range(2):
             ts("CG m%d" % j, "CGm", B["CGm"][:, 128 * j:128 * j + 128], B["CG"][:], sm("m%d" % j), None, A.mult)
         cp("PB4u", "Ui", B["Ui"][:], U[:, 0:256])
@@ -338,26 +383,19 @@ def rank_program(g, core, T, topo):
         if t:
             newcols(t - 1)
 
-        def ovcount(b):
-            mms("OV%d BD" % b, "PB6o", [(PB6[c32[b], k:128:16], B["OV"][:, 2 * b:2 * b + 2, k:256:16], bd8, True, True) for k in range(16)])
 
         def eqmat(h):
             for a in (2 * h, 2 * h + 1):
                 o = PD[h][:, 256 * (a % 2):256 * (a % 2) + 256]
                 mms("CG CGm NEG Id", "PD%d" % h, [(o, B["Id"][:], B["NEG"][:], True, False)])
-                if a % 2:
-                    wait("P", [("sP", cnt["P"] - 1)])
-                mms("CG CGm", "PD%d" % h, [(o, B["CG"][32 * a:32 * a + 32, :], B["CGm"][32 * a:32 * a + 32, :], False, True)])
+                mms("CG CGm" + (" rt%d" % h if a % 2 else ""), "PD%d" % h + ("" if a % 2 else " rt%d" % h), [(o, B["CG"][32 * a:32 * a + 32, :], B["CGm"][32 * a:32 * a + 32, :], False, True)])
 
         def eqact(h):
-            act("PD%d" % h, "EQ%d" % h, B["EQ"][:, 512 * h:512 * h + 512], PD[h][:], F.Relu, bias=-10.0)
+            act("PD%d" % h, "EQ%d" % h, B["EQ"][:, 512 * h:512 * h + 512], PD[h][:], F.Relu, bias=-15.0)
         for n, b in enumerate(order):
             act("PD%d" % b, "OV%d" % b, B["OV"][:, 2 * b:2 * b + 2, :], PD[b][:], F.Sign, bias=0.5)
-            if n == 1:
-                op("P", "hf IF", "PB4h", lambda: PE.transpose(U[:, 256:384], B["hf"][:], B["IF"][:, 0:128]))
-            ovcount(b)
-            if b == 0:
-                eqmat(0)
+        eqmat(0)
+        op("P", "hf IF", "PB4h", lambda: PE.transpose(U[:, 256:384], B["hf"][:], B["IF"][:, 0:128]))
         if t:
             cp("PB4h", "H16", B["H16"][:], U[:, 256:384])
         else:
@@ -367,9 +405,10 @@ def rank_program(g, core, T, topo):
         bk = B["bk"][:] if t else B["bk"][:, 0:H]
         BK = "bk0 bk1 bk2" if t else "bk0"
         eqmat(1)
+        mms("OV0 OV1 OV2 OV3 BD", "PB6o", [(PB6[:, k:128:16], B["OV"][:, :, k:256:16], bd8, True, True) for k in range(16)])
+        cp("OV0 OV1 OV2 OV3", "WO", B["WO"][:], B["OV"][:, :, 0:256:17])
+        mms("WO BD", "PB6o", [(PB6[:, 128:256], B["WO"][:], B["BD"][:], True, True)])
         mms("Cf IF", "PB5", [(KS[:, 0:256], B["Cf"][:], B["IF"][:], True, False)])
-        for b in sb:
-            mms("one CK", "PB5", [(KS[c32[b], 0:256], B["one"][:, 0:32], B["CK"][:], False, False)])
         def sbook(b):
             act(BK + " H16", "BC%d" % b, B["BC"][:, ch[b]], bk.indirect(B["H16"][:, c32[b]]), F.Copy)
 
@@ -380,58 +419,53 @@ def rank_program(g, core, T, topo):
         def bdiff(b):
             mms("Id nId BC%d D%d" % (b, b), "PD%d" % b, [(PD[b][:], B["Id"][:], B["BC"][:, ch[b]], True, False), (PD[b][:], B["nId"][:], B["D"][:, ch[b]], False, True)])
 
-        def count(b):
-            mms("IN%d RB RBh" % b, "PB5", [(KS[c32[b], k:256:16], B["IN"][:, 2 * b:2 * b + 2, k:256:16], B["RBh" if b in sb else "RB"][:], False, False) for k in range(16)])
+        def count(b0, b1):
+            mms(" ".join("IN%d" % b for b in range(b0, b1)) + " RB", "PB5",
+                [(KS[32 * b0:32 * b1, k:256:16], B["IN"][:, 2 * b0:2 * b1, k:256:16], B["RB"][:], False, False) for k in range(16)])
+        def answer():
+            act(BK + " ql%d" % t, "ys%d" % t, B["ys"][:, L * t:L * t + L], bk.indirect(B["ql"][:, 8 * t:8 * t + 8]), F.Copy)
+            send("ys%d" % t, "yl%d" % t, B["yl"][:, L * t:L * t + L], B["ys"][:, L * t:L * t + L], T.cores[qf], "ya%d" % t, "yo%d" % t,
+                 len(topo.engines(T.cores[qb], core)))
+        if t:
+            answer()
         sbook(sb[0])
-        act(BK + " ql%d" % t, "ys%d" % t, B["ys"][:, L * t:L * t + L], bk.indirect(B["ql"][:, 8 * t:8 * t + 8]), F.Copy)
-        wait("G", deps("G", ["ys%d" % t], []))
-        rid, pid = topo.addr(T.cores[qf], core)
-        g.remote_dma(B["yl"][:, L * t:L * t + L], B["ys"][:, L * t:L * t + L], T.sem["ya%d" % t], T.sem["yo%d" % t], pid, rid, topo.mask(core, T.cores[qf]))
-        lastw["yl%d" % t] = ("rem", ("ya%d" % t, len(topo.engines(T.cores[qb], core))))
+        act("PB6o", "ov", B["ov"][:], PB6[:, 0:256], F.Relu, scale=-64.0, bias=128.0)
+        if t == 0:
+            answer()
         for b in sb[1:]:
             sbook(b)
         eqact(0)
         vbook(vbk[0])
+        bdiff(sb[0])
         if t == 0:
             late_consts()
-        op("V", ER + " lst", "evf", lambda: V.tensor_copy(B["evf"][:], B["E"][:, 128:128 + wg].indirect(v16)))
-        tt("evf Ci", "d4", B["d4"][:], B["evf"][:], B["Ci"][:], A.subtract)
-        tt("d4 P", "d4P", B["d4P"][:], B["d4"][:], B["P"][:], A.mult)
-        tt("fe P", "feP", B["feP"][:], B["fe"][:], B["P"][:], A.mult)
-        cp("OV0 OV1 OV2 OV3", "WO", B["WO"][:], B["OV"][:, :, 0:256:17])
-        mms("WO BD", "PB6o", [(PB6[:, 128:256], B["WO"][:], B["BD"][:], True, True)])
         mms("d4 Iq fe Id d4P BDq feP BD16", "PB6k",
             [(PB6[:, 256:384], B["d4"][:], B["Iq"][:], True, False), (PB6[:, 256:384], B["fe"][:], B["Id"][:], False, True),
              (PB6[:, 384:512], B["d4P"][:], B["BDq"][:], True, False), (PB6[:, 384:512], B["feP"][:], B["BD16"][:], False, True)])
-        act("PB6o", "ov", B["ov"][:], PB6[:, 0:256], F.Relu, scale=-64.0, bias=128.0)
-        bdiff(sb[0])
-        count(vbk[0])
         for b in vbk[1:]:
             vbook(b)
         for b in sb[1:]:
             bdiff(b)
         tt("PB6k ov", "Kc", B["Kc"][:], PB6[:, 256:512], B["ov"][:], A.add)
-        tt("evf Pb", "evP", B["evP"][:], B["evf"][:], B["Pb"][:], A.mult)
-        tt("P4 evP", "AAb", B["AA"][:, 128:256], B["P4"][:], B["evP"][:], A.subtract)
-        ts("Ci", "AAa", B["AA"][:, 0:128], B["Ci"][:], -4095.0, None, A.add)
+        tt("evf PB7", "evP", B["evP"][:], B["evf"][:], CPb, A.mult)
+        tt("PB7 evP", "AAb", B["AA"][:, 128:256], CP4, B["evP"][:], A.subtract)
         tt("c128 e2", "BWa", B["BW"][:, 0:8], sm("c128"), vf, A.add)
         if last:
-            cp("E E0 E1", "EF", B["EF"][:, 128:128 + M + L * t], B["E"][:, 128:128 + M + L * t])
-        for b in vbk[1:]:
-            count(b)
+            c = 128 + wg
+            cp("E1", "EFb", B["EF"][:, c:c + L], B["E"][:, c:c + L])
+            cp("E E0", "EF", B["EF"][:, 128:c], B["E"][:, 128:c])
+            dma("Y", "EFb", "", "out0", T.ykids[:, c - 128:c - 128 + L], B["EF"][:, c:c + L])
+        count(0, 2)
         for b in sb:
-            act("PD%d" % b, "IN%d" % b, B["IN"][:, 2 * b:2 * b + 2, :], PD[b][:], F.Sign, bias=0.5)
-        count(sb[0])
-        for b in sb[1:]:
-            count(b)
-        mms("fe I14", "PB5", [(KS[:, 0:256], B["fe"][:], B["I14"][:], False, True)])
+            ts("PD%d" % b, "IN%d" % b, B["IN"][:, 2 * b:2 * b + 2, :], PD[b][:], 0.0, None, A.is_ge)
         eqact(1)
-        for b in vbk:
-            cp("IN%d" % b, "WI", B["WI"][:, c32[b]], B["IN"][:, 2 * b:2 * b + 2, 0:256:17])
-        for b in sb:
-            ts("IN%d" % b, "WI", B["WI"][:, c32[b]], B["IN"][:, 2 * b:2 * b + 2, 0:256:17], 0.5, 0.5, A.mult, A.add)
-        mms("WI BD", "PB7s", [(PM[:, 384:512], B["WI"][:], B["BD"][:], True, True)])
-        tt("PB7s Kc", "wr", B["wr"][:], PM[:, 384:512], B["Kc"][:, 128:256], A.is_gt)
+        act("Cf cb", "AAa", B["AA"][:, 0:128], B["Cf"][:], F.Identity, bias=sm("cb"))
+        count(2, 3)
+        cp("IN0 IN1 IN2 IN3", "WI", B["WI"][:], B["IN"][:, :, 0:256:17])
+        mms("WI BD", "PD2s", [(PD[2][:, 128:256], B["WI"][:], B["BD"][:], True, True)])
+        count(3, 4)
+        mms("fe I14 I14z", "PB5", [(KS[:, 0:256], B["fe"][:], B["I14"][:], False, True)])
+        tt("PD2s Kc", "wr", B["wr"][:], PD[2][:, 128:256], B["Kc"][:, 128:256], A.is_gt)
         mms("nIh wr EQ0 EQ1", "PD0w", [(PD[0][:, 0:128], B["nIh"][:], B["wr"][:], True, False)]
             + [(PD[0][:, 16 * k:16 * k + 16], B["EQ"][:, 128 * k:128 * k + 128], B["wr"][:, 16 * k:16 * k + 16], False, False) for k in range(8)]
             + [(PD[0][:, 0:128], B["nIh"][:], B["wr"][:], False, True)])
@@ -440,62 +474,118 @@ def rank_program(g, core, T, topo):
         tt("PB5 cap", "scap", B["scap"][:], sK, B["cap"][:], A.mult)
         tt("PB5 Kc", "nc", B["nc"][:], sK, B["Kc"][:, 0:128], A.is_le)
         op("V", "Mh scap", "scs", lambda: V.tensor_tensor_scan(B["scs"][:], B["Mh"][:], B["scap"][:], 0.0, A.mult, A.max))
-        for k in range(8):
+        for k in range(4):
             ts("P scs", "sp", B["sp"][:, 16 * k:16 * k + 16], B["P"][:, 0:16], B["scs"][:, 16 * k + 15:16 * k + 16], None, A.mult)
         tt("PB5 nc", "mk", B["mk"][:], KS[:, 0:128], B["nc"][:], A.mult)
         tt("PD0w TPm", "wP", B["wP"][:], PD[0][:, 0:128], B["TPm"][:], A.is_lt)
         op("V", "Mh mk", "sc", lambda: V.tensor_tensor_scan(B["sc"][:], B["Mh"][:], B["mk"][:], 0.0, A.mult, A.max))
         for k in range(8):
             ts("P sc", "zc", B["zc"][:, 16 * k:16 * k + 16], B["P"][:, 0:16], B["sc"][:, 16 * k + 15:16 * k + 16], None, A.mult)
-        tt("wr P", "wd", B["wd"][:], B["wr"][:], B["P"][:], A.mult)
+        tt("wr PB7", "wd", B["wd"][:], B["wr"][:], CP, A.mult)
         mms("Id nId x yl%d" % t, "PB4d", [(U[:, 256:384], B["Id"][:], x, True, False), (U[:, 256:384], B["nId"][:], B["yl"][:, L * t:L * t + L], False, True)])
         act("PB4d", "nx", nx, U[:, 256:384], F.Abs)
+        for k in range(4, 8):
+            act("P scs", "sp4", B["sp"][:, 16 * k:16 * k + 16], B["P"][:, 0:16], F.Copy, scale=B["scs"][:, 16 * k + 15:16 * k + 16])
         act("PD0w", "wL", B["wL"][:], PD[0][:, 0:128], F.Relu, scale=-1.0)
         mms("IF evP Pn P128 Id", "PB6v", [(PB6[:, 0:128], B["IF"][:, 0:128], B["evP"][:], True, False), (PB6[:, 0:128], B["IF"][:, 0:128], B["Pn"][:], False, False)]
             + [(PB6[:, 0:128], B["Id"][:], B["P128"][:], False, False)] * t)
         mms("cap Id", "PD3c", [(PD[3][:, 0:128], B["cap"][:], B["Id"][:], True, True)])
-        mms("sp I4", "PB6v", [(PB6[:, 0:128], B["sp"][:], B["I4"][:], False, True)])
-        mms("LW nx", "PB4b", [(U[:, 384:392], B["LW"][:, 128 * r:128 * r + 128], B["XX"][:, r:128:16], r == 0, r == 15) for r in range(16)])
-        cp("PB4b", "bk1", sm("bk1"), U[:, 384:392])
-        ts("bk1", "bk2", sm("bk2"), sm("bk1"), R - 1, None, A.bitwise_and)
-        tt("bk2 e2", "BWb", B["BW"][:, 8:16], sm("bk2"), vf, A.subtract)
-        mms("Id nx x one CA", "PB4a", [(U[:, 0:256], B["Id"][:], B["XX"][:], True, False), (U[:, 0:256], B["one"][:], B["CA"][:], False, False)])
+        mms("sp sp4 I4", "PB6v", [(PB6[:, 0:128], B["sp"][:], B["I4"][:], False, True)])
         mms("wP CH2", "PD2l", [(PD[2][:, 0:16], B["wP"][:], B["CH2"][:], True, True)])
         mms("zc BDf", "PD2l", [(PD[2][:, 24:32], B["zc"][:], B["BDf"][:], True, True)])
         mms("wd CH2", "PD2l", [(PD[2][:, 16:24], B["wd"][:], B["CH2"][:, 0:8], True, True)])
+        cp("PD2l", "ch1", sm("ch1"), PD[2][:, 24:32])
+        ts("ch1", "ch2", sm("ch2"), sm("ch1"), 2047, None, A.bitwise_and)
+        tt("e2 ch2", "ch3", sm("ch3"), vf, sm("ch2"), A.subtract)
+        tt("PD2l ch3", "ch4", sm("ch4"), PD[2][:, 16:24], sm("ch3"), A.mult)
+        tt("ch2 ch4", "BBb", B["BB"][:, 8:16], sm("ch2"), sm("ch4"), A.add)
+        tt("PD3c AAb", "mmb", B["mm"][:, 128:256], PD[3][:, 0:128], B["AA"][:, 128:256], A.mult)
+        tt("PB6v mmb", "VC", B["VC"][:], PB6[:, 0:128], B["mm"][:, 128:256], A.add)
+        mms("LW nx", "PD1b", [(PD[1][:, 128:136], B["LW"][:, 128 * r:128 * r + 128], B["XX"][:, r:128:16], r == 0, r == 15) for r in range(16)])
+        cp("PD1b", "bk1", sm("bk1"), PD[1][:, 128:136])
+        ts("bk1", "bk2", sm("bk2"), sm("bk1"), R - 1, None, A.bitwise_and)
+        tt("bk2 e2", "BWb", B["BW"][:, 8:16], sm("bk2"), vf, A.subtract)
+        mms("Id nx x one CA", "PB4a", [(U[:, 0:256], B["Id"][:], B["XX"][:], True, False), (U[:, 0:256], B["one"][:], B["CA"][:], False, False)])
         mms("wL JJ", "PB4a", [(U[:, 0:256], B["wL"][:], B["JJ"][:], False, True)])
         mms("x Id one CA wL JJ", "PD1x", [(PD[1][:, 0:128], B["Id"][:], x, True, False), (PD[1][:, 0:128], B["one"][:], B["CA"][:, 0:128], False, False),
                                           (PD[1][:, 0:128], B["wL"][:], B["JJ"][:, 0:128], False, True)])
         mms("cap scap wL Id I4", "PB5n", [(KS[:, 0:128], B["cap"][:], B["Id"][:], True, True), (KS[:, 128:256], B["scap"][:], B["I4"][:], True, True),
                                           (KS[:, 256:384], B["wL"][:], B["Id"][:], True, True)])
         act("PB4a", "xm", B["xm"][:], U[:, 0:256], F.Relu)
-        act("PD1x", "X", B["X"][:, M + L * t:M + L * t + L], PD[1][:, 0:128], F.Relu)
+        act("PD1x", "Xz X%d" % t, B["X"][:, M + L * t:M + L * t + L], PD[1][:, 0:128], F.Relu)
         if not last:
-            mms("xm Id", "PB7x", [(PM[:, 256:384], B["xm"][:, 0:128], B["Id"][:], True, False), (PM[:, 256:384], B["xm"][:, 128:256], B["Id"][:], False, True)])
-        mms("xm Id", "PB4x", [(U[:, 256:384], B["Id"][:], B["xm"][:, 0:128], True, False), (U[:, 256:384], B["Id"][:], B["xm"][:, 128:256], False, True)])
-        if not last:
-            act("PB7x", "xT", B["xT"][:], PM[:, 256:384], F.Copy)
-        act("PB4x", "x", x, U[:, 256:384], F.Copy)
-        tt("PD3c AAb", "mmb", B["mm"][:, 128:256], PD[3][:, 0:128], B["AA"][:, 128:256], A.mult)
-        cp("PD2l", "ch1", sm("ch1"), PD[2][:, 24:32])
-        ts("ch1", "ch2", sm("ch2"), sm("ch1"), 2047, None, A.bitwise_and)
-        tt("e2 ch2", "ch3", sm("ch3"), vf, sm("ch2"), A.subtract)
-        tt("PD2l ch3", "ch4", sm("ch4"), PD[2][:, 16:24], sm("ch3"), A.mult)
-        tt("ch2 ch4", "BBb", B["BB"][:, 8:16], sm("ch2"), sm("ch4"), A.add)
+            mms("xm Id", "PB4y", [(U[:, 384:512], B["xm"][:, 0:128], B["Id"][:], True, False), (U[:, 384:512], B["xm"][:, 128:256], B["Id"][:], False, True)])
+            act("PB4y", "xT", B["xT"][:], U[:, 384:512], F.Copy)
+        else:
+            newx()
         tt("PD2l BWa BWb", "e1", sm("e1"), PD[2][:, 0:16], B["BW"][:], A.mult)
         tt("e1 BBa BBb", "e2", B["e2"][:], sm("e1"), B["BB"][:], A.add)
         cp("e2", "lst", B["lst"][:], B["e2"][:])
-        tt("PB6v mmb", "VC", B["VC"][:], PB6[:, 0:128], B["mm"][:, 128:256], A.add)
         if not last:
-            op("V", "lst VC", ER, lambda: V.tensor_copy(B["E"][:, 0:128 + wg].indirect(B["lst"][:, 0:8]), B["VC"][:]))
+            nodes_at(t + 1)
+        if not last:
+            op("V", "lst VC", ER, lambda wg=wg: V.tensor_copy(B["E"][:, 0:128 + wg].indirect(B["lst"][:, 0:8]), B["VC"][:]))
         else:
             op("V", "lst VC EF", "EF", lambda: V.tensor_copy(B["EF"][:, 0:128 + wg].indirect(B["lst"][:, 0:8]), B["VC"][:]))
-            dma("Y", "EF", "", "out", T.ykids[:, 0:M + L * t], B["EF"][:, 128:128 + M + L * t])
+            dma("Y", "EF", "", "out", T.ykids[:, 0:wg], B["EF"][:, 128:128 + wg])
             newcols(t)
             dma("Y", "EF%d" % t, "", "out", T.ykids[:, M + L * t:M + L * t + L], B["EF"][:, 128 + M + L * t:128 + M + L * t + L])
-            dma("S", "X", "", "out", T.ynodes[:], B["X"][:, M:M + L * STEPS])
+            dma("S", XR + " X%d" % t, "", "out", T.ynodes[:], B["X"][:, M:M + L * STEPS])
             dma("S", "x", "", "out", T.ycand[:], x)
             dma("S", "e2", "", "out", T.yspot[:], vf)
+    def schedule():
+        N = len(calls)
+        WAKE, LOOK = TUNE["wake"], TUNE["look"]
+        noise = np.random.RandomState(TUNE["seed"]).rand(N) * TUNE["noise"]
+        succ = [[] for _ in range(N)]
+        left = [len(c["pre"]) for c in calls]
+        for c in calls:
+            for m in c["pre"]:
+                succ[m].append(c["n"])
+        prio = [0.0] * N
+        for n in range(N - 1, -1, -1):
+            c = calls[n]
+            prio[n] = c["dur"] + c["lat"] + max([prio[m] + (WAKE if calls[m]["pre"][n] else 0.0) for m in succ[n]] or [0.0])
+        for n in range(N):
+            prio[n] += float(noise[n])
+        free, end, start, est = {}, [0.0] * N, [0.0] * N, {}
+        for n in range(N):
+            if not left[n]:
+                est[n] = 0.0
+        out = []
+        while est:
+            at = {n: max(e, free.get(calls[n]["eng"], 0.0)) for n, e in est.items()}
+            lo = min(at.values())
+            n = max((m for m in at if at[m] <= lo + LOOK), key=lambda m: (prio[m], -m))
+            c = calls[n]
+            start[n] = at[n]
+            if c["eng"] != "A":
+                free[c["eng"]] = at[n] + c["dur"]
+            end[n] = at[n] + c["dur"] + c["lat"]
+            del est[n]
+            out.append(n)
+            for m in succ[n]:
+                left[m] -= 1
+                if not left[m]:
+                    est[m] = max(end[q] + WAKE if w else start[q] + calls[q]["dur"] for q, w in calls[m]["pre"].items())
+        return out
+
+    if "order" not in ORDERS:
+        ORDERS["order"] = schedule()
+    for n in ORDERS["order"]:
+        c = calls[n]
+        eng = c["eng"]
+        if eng == "A":
+            snap[c["tok"]] = {}
+            continue
+        wait(eng, [calls[m]["tok"] for m, w in c["pre"].items() if w])
+        i = c["fn"]()
+        if c["kind"] == "c":
+            cnt[eng] += 1
+            i.then_inc(T.sem["s" + eng], 1)
+            c["tok"] = ("s" + eng, cnt[eng])
+        if c["tok"]:
+            snap[c["tok"]] = dict(known[eng])
     for t in range(STEPS):
         for s in ("qo", "yo"):
             g.wait_ge(T.sem[s + str(t)], neng)

import numpy as np
from concourse.mybir import AluOpType as A, ActivationFunctionType as F

M, L, STEPS, H, R, NB = 896, 128, 3, 2048, 512, 4
XW = 1296
SBANKS = (2, 3)
XS = (1, 2)

BF, F32, I32, U16 = "bfloat16", "float32", "int32", "uint16"
_S = {
    "spi": (8, I32), "E": (128 + 1280, I32), "EF": (128 + 1280, F32), "X": (XW, BF), "bk": (3 * H, BF), "XX": (2 * L, BF),
    "wt": (2, BF), "wl0": (2, BF), "wl1": (2, BF), "wl2": (2, BF),
    "qs": (8 * STEPS, U16), "ql": (8 * STEPS, U16), "ys": (L * STEPS, BF), "yl": (L * STEPS, BF),
    "one": (128, BF), "zer": (256, BF), "pk": (128, I32), "Id": (128, BF), "nId": (128, BF), "IF": (256, F32), "JJ": (256, BF), "CA": (256, BF),
    "BD0": (128, BF), "BD": (128, BF), "BDf": (8, F32), "P": (128, BF), "Pb": (128, BF), "P4": (128, F32), "P128": (128, BF), "TPm": (128, BF),
    "NEG": (256, BF), "I4": (128, BF), "Iq": (128, BF), "I14": (256, BF), "nIh": (128, BF), "BDq": (128, BF), "BD16": (128, BF), "CH2": (16, BF),
    "RB": (16, BF), "WO": (128, BF), "WI": (128, BF), "Ex": (2048, BF), "Mh": (128, BF), "W": (16, BF), "Wz": (48, BF),
    "LW": (2048, BF), "lwo": (2, U16), "wrep": (16, BF), "chp": (8, BF),
    "ni": (128, F32), "Pn": (128, F32), "pt": (128, I32), "ptb": (256, BF), "lowb": (128, BF), "hib": (16, F32), "CODE": (1280, BF),
    "lst": (16, U16), "e2": (16, F32), "BW": (16, F32), "BB": (16, F32),
    "Ci": (128, I32), "C16": (128, U16), "XC": (2048, BF), "D": (2048, BF), "xT": (128, BF), "XV": (128, BF), "z": (128, BF), "zh": (128, F32),
    "Ui": (256, I32), "U2": (256, I32), "h1": (128, I32), "h2": (128, I32), "hf": (128, F32), "H16": (128, U16), "BC": (2048, BF),
    "CG": (128, BF), "CGm": (256, BF), "EQ": (1024, BF), "evf": (128, F32), "d4": (128, BF), "fe": (128, BF), "d4P": (128, BF), "feP": (128, BF),
    "Cf": (128, F32), "AA": (256, F32), "evP": (128, F32), "Kc": (256, F32), "ov": (256, F32), "xm": (256, BF),
    "wr": (128, BF), "wd": (128, BF), "cap": (128, BF), "nc": (128, F32), "mk": (128, F32), "sc": (128, F32), "zc": (128, F32),
    "scap": (128, BF), "scs": (128, F32), "sp": (128, BF), "wP": (128, BF), "wL": (128, BF),
    "mm": (256, F32), "VC": (128, F32), "n1": (128, F32), "n2": (128, F32),
    "i8": (128, I32), "f8": (128, F32),
}
SCRATCH = {k: ("sbuf", [128, w], d) for k, (w, d) in _S.items()}
for _k in ("OV", "IN"):
    SCRATCH[_k] = ("sbuf", [128, 8, 256], BF)
for _k in ("PD0", "PD1", "PD2", "PD3", "PB4", "PB5", "PB6", "PB7"):
    SCRATCH[_k] = ("psum", [128, 512], F32)
_I8 = {"uz": (0, 16), "uz2": (16, 16), "hz1": (32, 8), "hz2": (40, 8), "bk1": (48, 8), "bk2": (56, 8), "ch1": (64, 8), "ch2": (72, 8),
       "ip": (80, 1), "p15": (84, 1), "mi": (88, 1), "g8": (96, 8)}
_F8 = {"hz": (0, 8), "ch3": (8, 8), "ch4": (16, 8), "il": (24, 8), "c128": (32, 8), "e1": (40, 16), "lwi": (56, 1), "colk": (60, 1), "m0": (64, 1),
       "m1": (68, 1), "lwf": (72, 1), "cb": (76, 1)}
SLICED = set("pt Ex W JJ I14 CH2 RB RBh CK CA ptb zh zc sp IF WI CGm Wz CODE IN0 IN1 IN2 IN3 PB7".split())
DUR = {"V": 0.13, "S": 0.19, "P": 0.13, "G": 0.4, "Y": 0.1, "A": 0.0}
COST = {"VCi": 0.24, "VXC": 0.82, "Vevf": 0.24, "VXV": 0.24, "VE": 0.43, "VEF": 0.43, "VUi": 0.26, "VU": 0.26, "Vh": 0.26, "Vhf": 0.26, "VIN": 0.47,
        "Vd": 0.26, "VKc": 0.26, "VLW": 0.1, "SD": 0.57, "SOV": 0.57, "SEQ": 0.57, "SXC": 0.82, "SBC": 0.82, "Sov": 0.32, "Sxm": 0.32, "SCG": 0.25,
        "Sys": 0.25, "PPD": 0.26, "PPDw": 0.38, "PPB": 0.4, "PPBu": 0.5, "PPBh": 0.26, "PPBo": 0.3, "PPBk": 0.26, "PPBv": 0.3, "PPDb": 0.52}
for _k in ("uz", "uz2", "hz1", "hz2", "hz", "zh", "qs", "zc", "sp", "ch1", "ch2", "ch3", "ch4", "BBb", "BWa", "BWb", "bk1", "bk2", "e1", "e2", "lst", "WI", "WO",
           "CODE", "Ex", "W", "Wz", "RB", "CH2", "nId", "pt", "ptb", "CGm", "lwi", "lwf", "lwo", "il", "c128", "BBa", "BDf", "p15", "colk", "m0", "m1", "mi",
           "chp", "wrep", "Pb"):
    COST["V" + _k.rstrip("0123456789")] = 0.065
COST["Sspk"] = COST["Spsk"] = 0.13
TUNE = {"wake": 0.13, "remote": 2.5, "look": 0.02, "noise": 0.1, "seed": 9594}
ORDERS = {}
DMAS = ["spi", "E", "x", "X", "wt", "bk0", "bk1", "bk2", "out", "out0"]
SEMAPHORES = (["sV", "sS", "sP", "sG", "wloc", "wrem"] + ["d_" + k for k in DMAS]
              + [k + str(t) for k in ("qa", "qo", "ya", "yo") for t in range(STEPS)])


def rank_program(g, core, T, topo):
    rank = T.rank_of(core)
    if rank is None:
        return
    Q = {"V": g.vector, "S": g.scalar, "P": g.tensor, "G": g, "Y": g.sync}
    cnt = {k: 0 for k in "VSPG"}
    known = {k: {} for k in Q}
    snap = {}
    lastw, readers, banks = {}, {}, {}
    B = {k: T[k] for k in SCRATCH}

    def sm(k, a=0, b=None):
        buf, (o, w) = ("i8", _I8[k]) if k in _I8 else ("f8", _F8[k])
        return B[buf][:, o + a:o + (w if b is None else b)]

    def wait(eng, toks):
        best = {}
        for s, v in toks:
            if known[eng].get(s, 0) < v:
                best[s] = max(best.get(s, 0), v)
        for s, v in sorted(best.items(), key=lambda a: -len(snap.get(a, ()))):
            if known[eng].get(s, 0) >= v:
                continue
            Q[eng].wait_ge(T.sem[s], v)
            known[eng][s] = v
            for a, b in snap.get((s, v), {}).items():
                known[eng][a] = max(known[eng].get(a, 0), b)

    calls = []

    def note(eng, rd, wr, fn, kind="c", dur=None, lat=0.0, tok=None):
        rd, wr = rd.split(), wr.split()
        n, pre = len(calls), {}

        def edge(m, w):
            pre[m] = pre.get(m, False) or w
        for k in rd:
            for m in lastw.get(k, ()):
                edge(m, True)
        for k in wr:
            old, rs = lastw.get(k, []), readers.get(k, [])
            if k in SLICED and old and not rs and calls[old[0]]["eng"] == eng:
                lastw[k] = old + [n]
                for m in calls[old[0]]["pre"]:
                    if calls[old[0]]["pre"][m]:
                        edge(m, True)
                continue
            for m in old:
                edge(m, not (eng == "P" and calls[m]["eng"] == "P"))
            for m in rs:
                edge(m, not (eng == "P" and calls[m]["eng"] == "P"))
            lastw[k], readers[k] = [n], []
        for k in rd:
            readers.setdefault(k, []).append(n)
        for k in sorted(set(k[:3] for k in rd + wr if k[:2] in ("PD", "PB"))):
            cur, prev = banks.get(k, (None, [])), None
            if cur[0] != eng:
                banks[k] = cur = (eng, [], cur[1])
            for m in cur[2]:
                edge(m, True)
            if eng == "P":
                for m in cur[1]:
                    edge(m, False)
            cur[1].append(n)
        calls.append({"eng": eng, "pre": pre, "fn": fn, "kind": kind, "lat": lat, "tok": tok, "n": n,
                      "dur": dur if dur is not None else COST.get(eng + wr[0].rstrip("0123456789"), DUR[eng])})
        return n

    def op(eng, rd, wr, fn, dur=None):
        return note(eng, rd, wr, fn, dur=dur)

    dcount = {}

    def dma(eng, rd, wr, sem, out, in_, lat=3.0):
        dcount[sem] = dcount.get(sem, 0) + 16
        note(eng, rd, wr, lambda: Q[eng].dma_start(out, in_).then_inc(T.sem["d_" + sem], 16), "d", 0.1, lat, ("d_" + sem, dcount[sem]))

    def send(rd, wr, out, in_, dst, arrive, left, lands):
        rid, pid = topo.addr(dst, core)
        m = note("G", rd, "", lambda: g.remote_dma(out, in_, T.sem[arrive], T.sem[left], pid, rid, topo.mask(core, dst)), "r", 0.4)
        if wr:
            n = note("A", "", wr, None, "a", 0.0, TUNE["remote"], (arrive, lands))
            calls[n]["pre"][m] = True

    V, S, PE = g.vector, g.scalar, g.tensor

    def tt(rd, wr, out, a, b, o):
        op("V", rd, wr, lambda: V.tensor_tensor(out, a, b, o))

    def ts(rd, wr, out, a, s1, s2, o0, o1=None):
        if o1 is None:
            op("V", rd, wr, lambda: V.tensor_scalar(out, a, s1, s2, o0))
        else:
            op("V", rd, wr, lambda: V.tensor_scalar(out, a, s1, s2, o0, o1))

    def cp(rd, wr, out, a):
        op("V", rd, wr, lambda: V.tensor_copy(out, a))

    def act(rd, wr, out, a, f, **kw):
        op("S", rd, wr, lambda: S.activation(out, a, f, **kw))

    def mms(rd, wr, lst):
        def go():
            i = None
            for out, l, r, st, sp in lst:
                i = PE.matmul(out, l, r, st, sp)
            return i
        op("P", rd, wr, go)

    def memset(wr, ap, c):
        op("V", "", wr, lambda: V.memset(ap, c))

    nx, x = B["XX"][:, 0:L], B["XX"][:, L:2 * L]
    dma("Y", "", "spi", "spi", B["spi"][:], T.spot[:])
    dma("Y", "", "E", "E", B["E"][:, 128:128 + M], T.kids[:])
    dma("S", "", "wt", "wt", B["wt"][:], T.wts[:])
    dma("S", "", "x", "x", x, T.cand[:])
    dma("S", "", "X", "X", B["X"][:, 0:M], T.nodes[:])
    for j in range(3):
        dma("Y", "", "bk%d" % j, "bk%d" % j, B["bk"][:, H * j:H * j + H], T.book[:])

    memset("one", B["one"][:], 1.0)
    memset("zer", B["zer"][:], 0.0)
    op("G", "one", "Id", lambda: g.affine_select(B["Id"][:], B["one"][:], [[-1, 128]], A.is_equal, 0.0, 0, 1))
    op("G", "one", "BD0", lambda: g.affine_select(B["BD0"][:], B["one"][:], [[-16, 8], [0, 16]], A.is_ge, 0.0, 0, 1))
    op("G", "BD0", "BD", lambda: g.affine_select(B["BD"][:], B["BD0"][:], [[16, 8], [0, 16]], A.is_ge, 0.0, 15, -1))
    op("G", "", "pk", lambda: g.iota(B["pk"][:], [[0, 8], [-1, 16]], 16, 1))
    op("G", "", "ip", lambda: g.iota(sm("ip"), [[0, 1]], 0, 1))
    op("G", "", "g8", lambda: g.iota(sm("g8"), [[0, 8]], 0, 1))
    neng = len(topo.engines(core, T.cores[(rank + 1) % NB]))
    for j in range(NB - 1):
        send("wt", "wl0 wl1 wl2" if j == NB - 2 else "", B["wl%d" % j][:], B["wt"][:], T.cores[(rank - 1 - j) % NB], "wrem", "wloc", neng * (NB - 1))
    op("G", "zer", "NEG", lambda: g.affine_select(B["NEG"][:], B["zer"][:], [[0, 2], [1, 128]], A.is_gt, -100.0, 0, -1))
    op("G", "", "ni", lambda: g.iota(B["ni"][:], [[1, 128]], M, 0, allow_small_or_imprecise_dtypes=True))
    op("G", "", "LW", lambda: g.iota(B["LW"][:], [[0, 2048]], 0, 0, allow_small_or_imprecise_dtypes=True))

    memset("Xz", B["X"][:, M:XW], 0.0)
    memset("ptb0", B["ptb"][:, 128:256], 0.0)
    memset("pt0", B["pt"][:], 0)
    memset("Mh", B["Mh"][:], 1.0)
    memset("Mh", B["Mh"][:, 0:128:16], 0.0)
    memset("IF", B["IF"][:, 128:256], 0.0)
    memset("CA", B["CA"][:, 0:128], -2.0)
    memset("CA", B["CA"][:, 128:256], 0.0)
    bd8 = B["BD"][:, 0:128:16]
    ts("Id", "nId", B["nId"][:], B["Id"][:], -1.0, None, A.mult)
    mms("x Id", "PB4x", [(B["PB4"][:, 384:512], x, B["Id"][:], True, True)])
    act("PB4x", "xT", B["xT"][:], B["PB4"][:, 384:512], F.Copy)
    EXR = "Ex"
    for k in range(16):
        if k % 3 == 2:
            act("Id", "Ex%d" % k, B["Ex"][:, k:2048:16], B["Id"][:], F.Copy)
            EXR += " Ex%d" % k
        else:
            cp("Id", "Ex", B["Ex"][:, k:2048:16], B["Id"][:])
    ts("pk", "Ci", B["Ci"][:], B["pk"][:], 15, None, A.bitwise_and)
    ts("Ci", "P", B["P"][:], B["Ci"][:], 0, None, A.is_equal)
    cp("Id", "IF", B["IF"][:, 0:128], B["Id"][:])
    cp("BD", "BDf", B["BDf"][:], bd8)
    ts("ip", "p15", sm("p15"), sm("ip"), 15, None, A.bitwise_and)
    ts("p15", "colk", sm("colk"), sm("p15"), -2048.0, 30720.0, A.mult, A.add)
    ts("P", "Pb", B["Pb"][:], B["P"][:], -1.0, 1.0, A.mult, A.add)
    CP, CPb, CP4 = (B["PB7"][:, 128 * j:128 * j + 128] for j in range(3))
    cp("P", "PB7", CP, B["P"][:])
    cp("Pb", "PB7", CPb, B["Pb"][:])
    ts("Pb", "PB7", CP4, B["Pb"][:], 4095.0, None, A.mult)
    act("P", "TPm", B["TPm"][:], B["P"][:], F.Copy, scale=1000.0, bias=-1000.0)
    act("colk", "cb", sm("cb"), sm("colk"), F.Copy, scale=-1.0, bias=-4095.0)
    for k, src, f in (("nIh", "Id", -0.5), ("I4", "Id", 4096.0), ("Iq", "Id", 1.0 / 4096), ("P128", "P", 128.0), ("BDq", "BD", 1.0 / 4096),
                      ("BD16", "BD", -16.0)):
        act(src, k, B[k][:], B[src][:], F.Copy, scale=f)
    memset("I14z", B["I14"][:, 128:256], 0.0)
    act("Id", "I14", B["I14"][:, 0:128], B["Id"][:], F.Copy, scale=-16384.0)
    for j in range(2):
        act("Id", "JJ", B["JJ"][:, 128 * j:128 * j + 128], B["Id"][:], F.Copy, scale=(256.0, -256.0)[j])
        cp("BD", "CH2", B["CH2"][:, 8 * j:8 * j + 8], bd8)
        ts("BD", "RB", B["RB"][:, 8 * j:8 * j + 8], bd8, (32768.0, 1.0)[j], None, A.mult)
    pt = B["pt"]
    for b in range(7):
        ts("g8 pt0", "pt", pt[:, b:128:16], sm("g8"), b, 1, A.logical_shift_right, A.bitwise_and)
    ts("pt", "ptb", B["ptb"][:, 0:128], pt[:], 2.0, -1.0, A.mult, A.add)
    for b in range(7, 11):
        ts("ptb0 pt", "ptb", B["ptb"][:, 128 + b:256:16], pt[:, b - 7:128:16], 2.0, None, A.mult)
    mms("ptb Id", "PB6c", [(B["PB6"][:, 256:384], B["ptb"][:, 0:128], B["Id"][:], True, True),
                           (B["PB6"][:, 384:400], B["ptb"][:, 128:256], B["Id"][:, 0:16], True, True)])
    act("PB6c", "hib", B["hib"][:], B["PB6"][:, 384:400], F.Copy)
    act("PB6c", "lowb", B["lowb"][:], B["PB6"][:, 256:384], F.Copy)
    ts("ip", "mi", sm("mi"), sm("ip"), 4, 1, A.logical_shift_right, A.bitwise_and)
    cp("mi", "m1", sm("m1"), sm("mi"))
    ts("m1", "m0", sm("m0"), sm("m1"), -1.0, 1.0, A.mult, A.add)
    cp("ip", "lwi", sm("lwi"), sm("ip"))
    ts("BD lwi", "chp", B["chp"][:], bd8, sm("lwi"), None, A.mult)
    mms("P chp", "PD3i", [(B["PD3"][:, 0:8], B["P"][:], B["chp"][:], True, True)])
    cp("PD3i", "il", sm("il"), B["PD3"][:, 0:8])
    ts("il", "c128", sm("c128"), sm("il"), -1.0, 128.0, A.mult, A.add)
    cp("il", "BBa", B["BB"][:, 0:8], sm("il"))
    for u in range(2):
        ts("BD wt", "W", B["W"][:, 8 * u:8 * u + 8], bd8, B["wt"][:, u:u + 1], None, A.mult)
    cp("spi", "lst", B["lst"][:, 8:16], B["spi"][:])
    cp("spi", "e2", B["e2"][:, 8:16], B["spi"][:])

    def code_blocks():
        for h in range(10):
            ts("lowb hib", "CODE", B["CODE"][:, 128 * h:128 * h + 128], B["lowb"][:], B["hib"][:, h:h + 1], None, A.add)

    def late_consts():
        tt("P ni", "Pn", B["Pn"][:], B["P"][:], B["ni"][:], A.mult)
        ts("p15 lwi", "lwf", sm("lwf"), sm("p15"), 128.0, sm("lwi"), A.mult, A.add)
        cp("lwf", "lwo", B["lwo"][:, 0:1], sm("lwf"))
        ts("one wt", "wrep", B["wrep"][:], B["one"][:, 0:16], B["wt"][:, 0:1], None, A.mult)
        op("V", "lwo wrep LW", "LW", lambda: V.tensor_copy(B["LW"][:].indirect(B["lwo"][:, 0:1]), B["wrep"][:]))

    PD = [B["PD%d" % b] for b in range(4)]
    U, KS, PB6 = B["PB4"], B["PB5"], B["PB6"]
    v16, vf = B["lst"][:, 8:16], B["e2"][:, 8:16]
    sb = list(SBANKS)
    vbk = [b for b in range(4) if b not in sb]
    vb = [b for b in range(4) if b not in XS]
    order = list(range(4))
    dorder = list(XS) + vb
    ch = [slice(512 * b, 512 * b + 512) for b in range(4)]
    c32 = [slice(32 * b, 32 * b + 32) for b in range(4)]

    def newcols(t):
        tt("PB5n AAa", "mma", B["mm"][:, 0:128], KS[:, 0:128], B["AA"][:, 0:128], A.mult)
        tt("PB5n mma", "n1", B["n1"][:], KS[:, 128:256], B["mm"][:, 0:128], A.add)
        tt("PB5n n1", "n2", B["n2"][:], KS[:, 256:384], B["n1"][:], A.mult)
        k = "EF" if t == STEPS - 1 else "E"
        c = 128 + M + L * t
        ts("n2", k + str(t), B[k][:, c:c + L], B["n2"][:], 4095.0, None, A.add)

    def nodes_at(t):
        op("V", "X lst " + " ".join("X%d" % j for j in range(t - 1)), "XV",
           lambda: V.tensor_copy(B["XV"][:], B["X"][:, 0:M + L * max(0, t - 1)].indirect(v16)))

    def newx():
        mms("xm Id", "PB4x", [(U[:, 256:384], B["Id"][:], B["xm"][:, 0:128], True, False), (U[:, 256:384], B["Id"][:], B["xm"][:, 128:256], False, True)])
        act("PB4x", "x", x, U[:, 256:384], F.Copy)

    for t in range(STEPS):
        last = t == STEPS - 1
        wg = M + L * max(0, t - 1)
        XR = "X Xz " + " ".join("X%d" % j for j in range(t))
        ER = "E " + " ".join("E%d" % j for j in range(t - 1))
        qb = (rank + 1 + t) % NB
        qf = (rank - 1 - t) % NB
        ts(ER + " lst", "Ci", B["Ci"][:], B["E"][:, 128:128 + wg].indirect(v16), 4095, None, A.bitwise_and)
        ts("Ci", "C16", B["C16"][:], B["Ci"][:], 1280.0, None, A.min)
        if t == 0:
            nodes_at(t)
        mms("XV xm Id nId x", "PB5z", [(KS[:, 384:512], B["Id"][:], B["XV"][:], True, False)]
            + ([(KS[:, 384:512], B["nId"][:], x, False, True)] if t == 0 else
               [(KS[:, 384:512], B["nId"][:], B["xm"][:, L * j:L * j + L], False, j == 1) for j in range(2)]))
        act("PB5z", "z", B["z"][:], KS[:, 384:512], F.Abs)
        if t:
            mms("z Wz", "PB5u", [(KS[:, 384:400], B["z"][:], B["Wz"][:, 16 * t:16 * t + 16], True, True)])
        for b in order:
            mms("%s xT" % EXR, "PD%d" % b, [(PD[b][:], B["xT"][:], B["Ex"][:, ch[b]], True, False)])

        def diff(b):
            mms("nId XC%d" % b, "PD%d" % b, [(PD[b][:], B["nId"][:], B["XC"][:, ch[b]], False, True)])

        def hashsum(b0, b1):
            mms(" ".join("D%d" % b for b in range(b0, b1)) + " W", "PB4u",
                [(U[32 * b0:32 * b1, k:256:16], B["D"][:, 512 * b0 + k:512 * b1:16], B["W"][:], True, True) for k in range(16)])

        for b in XS:
            act(XR + " C16", "XC%d" % b, B["XC"][:, ch[b]], B["X"][:].indirect(B["C16"][:, c32[b]]), F.Copy)
        if t:
            newx()
        if t == 0:
            for b in vb[:-1]:
                cp(XR + " C16", "XC%d" % b, B["XC"][:, ch[b]], B["X"][:].indirect(B["C16"][:, c32[b]]))
            for b in dorder[:-1]:
                diff(b)
            for j in range(3):
                for u in range(2):
                    ts("BD wl%d" % j, "Wz", B["Wz"][:, 16 * j + 8 * u:16 * j + 8 * u + 8], bd8, B["wl%d" % j][:, u:u + 1], None, A.mult)
            mms("z Wz", "PB5u", [(KS[:, 384:400], B["z"][:], B["Wz"][:, 16 * t:16 * t + 16], True, True)])
        cp("PB5u", "uz", sm("uz"), KS[:, 384:400])
        ts("uz", "uz2", sm("uz2"), sm("uz"), 4095, None, A.bitwise_and)
        tt("uz2", "hz1", sm("hz1"), sm("uz2", 0, 8), sm("uz2", 8, 16), A.mult)
        ts("hz1", "hz2", sm("hz2"), sm("hz1"), 5, H - 1, A.logical_shift_right, A.bitwise_and)
        if t:
            tt("hz2 uz2", "hz", sm("hz"), sm("hz2"), sm("uz2", 8, 16), A.add)
        else:
            tt("hz2 uz2", "hz1", sm("hz1"), sm("hz2"), sm("uz2", 8, 16), A.add)
            ts("hz1", "hz2", sm("hz2"), sm("hz1"), H - 1, None, A.bitwise_and)
            cp("hz2", "hz", sm("hz"), sm("hz2"))
        for k in range(8):
            ts("P hz", "zh", B["zh"][:, 16 * k:16 * k + 16], B["P"][:, 0:16], sm("hz", k, k + 1), None, A.mult)
        mms("zh BDf", "PB5q", [(KS[:, 400:408], B["zh"][:], B["BDf"][:], True, True)])
        if t:
            for b in XS:
                diff(b)
        ts("Ci", "fe", B["fe"][:], B["Ci"][:], 4095.0, 128.0, A.is_ge, A.mult)
        ts("Ci colk", "Cf", B["Cf"][:], B["Ci"][:], sm("colk"), None, A.add)
        cp("PB5q", "qs%d" % t, B["qs"][:, 8 * t:8 * t + 8], KS[:, 400:408])
        send("qs%d" % t, "ql%d" % t, B["ql"][:, 8 * t:8 * t + 8], B["qs"][:, 8 * t:8 * t + 8], T.cores[qb], "qa%d" % t, "qo%d" % t,
             len(topo.engines(T.cores[qf], core)))
        for b in vb if t else vb[-1:]:
            cp(XR + " C16", "XC%d" % b, B["XC"][:, ch[b]], B["X"][:].indirect(B["C16"][:, c32[b]]))
            if b != 3:
                diff(b)
        for n, b in enumerate(dorder):
            act("PD%d" % b, "D%d" % b, B["D"][:, ch[b]], PD[b][:], F.Abs)
            if n == 0 and t:
                act("CODE lst", "CG", B["CG"][:], B["CODE"][:].indirect(v16), F.Copy)
            if n == 1:
                diff(3)
            if n == 2:
                hashsum(0, 3)
        hashsum(3, 4)
        if t == 0:
            code_blocks()
            act("CODE lst", "CG", B["CG"][:], B["CODE"][:].indirect(v16), F.Copy)
        op("V", ER + " lst", "evf", lambda wg=wg: V.tensor_copy(B["evf"][:], B["E"][:, 128:128 + wg].indirect(v16)))
        tt("evf Ci", "d4", B["d4"][:], B["evf"][:], B["Ci"][:], A.subtract)
        tt("d4 PB7", "d4P", B["d4P"][:], B["d4"][:], CP, A.mult)
        tt("fe PB7", "feP", B["feP"][:], B["fe"][:], CP, A.mult)
        for j in range(2):
            ts("CG m%d" % j, "CGm", B["CGm"][:, 128 * j:128 * j + 128], B["CG"][:], sm("m%d" % j), None, A.mult)
        cp("PB4u", "Ui", B["Ui"][:], U[:, 0:256])
        ts("Ui", "U2", B["U2"][:], B["Ui"][:], 4095, None, A.bitwise_and)
        tt("U2", "h1", B["h1"][:], B["U2"][:, 0:128], B["U2"][:, 128:256], A.mult)
        ts("h1", "h2", B["h2"][:], B["h1"][:], 5, H - 1, A.logical_shift_right, A.bitwise_and)
        tt("h2 U2", "hf", B["hf"][:], B["h2"][:], B["U2"][:, 128:256], A.add)
        if t:
            newcols(t - 1)


        def eqmat(h):
            for a in (2 * h, 2 * h + 1):
                o = PD[h][:, 256 * (a % 2):256 * (a % 2) + 256]
                mms("CG CGm NEG Id", "PD%d" % h, [(o, B["Id"][:], B["NEG"][:], True, False)])
                mms("CG CGm" + (" rt%d" % h if a % 2 else ""), "PD%d" % h + ("" if a % 2 else " rt%d" % h), [(o, B["CG"][32 * a:32 * a + 32, :], B["CGm"][32 * a:32 * a + 32, :], False, True)])

        def eqact(h):
            act("PD%d" % h, "EQ%d" % h, B["EQ"][:, 512 * h:512 * h + 512], PD[h][:], F.Relu, bias=-15.0)
        for n, b in enumerate(order):
            act("PD%d" % b, "OV%d" % b, B["OV"][:, 2 * b:2 * b + 2, :], PD[b][:], F.Sign, bias=0.5)
        eqmat(0)
        op("P", "hf IF", "PB4h", lambda: PE.transpose(U[:, 256:384], B["hf"][:], B["IF"][:, 0:128]))
        if t:
            cp("PB4h", "H16", B["H16"][:], U[:, 256:384])
        else:
            cp("PB4h", "h1", B["h1"][:], U[:, 256:384])
            ts("h1", "h2", B["h2"][:], B["h1"][:], H - 1, None, A.bitwise_and)
            cp("h2", "H16", B["H16"][:], B["h2"][:])
        bk = B["bk"][:] if t else B["bk"][:, 0:H]
        BK = "bk0 bk1 bk2" if t else "bk0"
        eqmat(1)
        mms("OV0 OV1 OV2 OV3 BD", "PB6o", [(PB6[:, k:128:16], B["OV"][:, :, k:256:16], bd8, True, True) for k in range(16)])
        cp("OV0 OV1 OV2 OV3", "WO", B["WO"][:], B["OV"][:, :, 0:256:17])
        mms("WO BD", "PB6o", [(PB6[:, 128:256], B["WO"][:], B["BD"][:], True, True)])
        mms("Cf IF", "PB5", [(KS[:, 0:256], B["Cf"][:], B["IF"][:], True, False)])
        def sbook(b):
            act(BK + " H16", "BC%d" % b, B["BC"][:, ch[b]], bk.indirect(B["H16"][:, c32[b]]), F.Copy)

        def vbook(b):
            for c in (2 * b, 2 * b + 1):
                tt(BK + " H16 D%d" % b, "IN%d" % b, B["IN"][:, c, :], bk.indirect(B["H16"][:, 16 * c:16 * c + 16]), B["D"][:, 256 * c:256 * c + 256], A.is_ge)

        def bdiff(b):
            mms("Id nId BC%d D%d" % (b, b), "PD%d" % b, [(PD[b][:], B["Id"][:], B["BC"][:, ch[b]], True, False), (PD[b][:], B["nId"][:], B["D"][:, ch[b]], False, True)])

        def count(b0, b1):
            mms(" ".join("IN%d" % b for b in range(b0, b1)) + " RB", "PB5",
                [(KS[32 * b0:32 * b1, k:256:16], B["IN"][:, 2 * b0:2 * b1, k:256:16], B["RB"][:], False, False) for k in range(16)])
        def answer():
            act(BK + " ql%d" % t, "ys%d" % t, B["ys"][:, L * t:L * t + L], bk.indirect(B["ql"][:, 8 * t:8 * t + 8]), F.Copy)
            send("ys%d" % t, "yl%d" % t, B["yl"][:, L * t:L * t + L], B["ys"][:, L * t:L * t + L], T.cores[qf], "ya%d" % t, "yo%d" % t,
                 len(topo.engines(T.cores[qb], core)))
        if t:
            answer()
        sbook(sb[0])
        act("PB6o", "ov", B["ov"][:], PB6[:, 0:256], F.Relu, scale=-64.0, bias=128.0)
        if t == 0:
            answer()
        for b in sb[1:]:
            sbook(b)
        eqact(0)
        vbook(vbk[0])
        bdiff(sb[0])
        if t == 0:
            late_consts()
        mms("d4 Iq fe Id d4P BDq feP BD16", "PB6k",
            [(PB6[:, 256:384], B["d4"][:], B["Iq"][:], True, False), (PB6[:, 256:384], B["fe"][:], B["Id"][:], False, True),
             (PB6[:, 384:512], B["d4P"][:], B["BDq"][:], True, False), (PB6[:, 384:512], B["feP"][:], B["BD16"][:], False, True)])
        for b in vbk[1:]:
            vbook(b)
        for b in sb[1:]:
            bdiff(b)
        tt("PB6k ov", "Kc", B["Kc"][:], PB6[:, 256:512], B["ov"][:], A.add)
        tt("evf PB7", "evP", B["evP"][:], B["evf"][:], CPb, A.mult)
        tt("PB7 evP", "AAb", B["AA"][:, 128:256], CP4, B["evP"][:], A.subtract)
        tt("c128 e2", "BWa", B["BW"][:, 0:8], sm("c128"), vf, A.add)
        if last:
            c = 128 + wg
            cp("E1", "EFb", B["EF"][:, c:c + L], B["E"][:, c:c + L])
            cp("E E0", "EF", B["EF"][:, 128:c], B["E"][:, 128:c])
            dma("Y", "EFb", "", "out0", T.ykids[:, c - 128:c - 128 + L], B["EF"][:, c:c + L])
        count(0, 2)
        for b in sb:
            ts("PD%d" % b, "IN%d" % b, B["IN"][:, 2 * b:2 * b + 2, :], PD[b][:], 0.0, None, A.is_ge)
        eqact(1)
        act("Cf cb", "AAa", B["AA"][:, 0:128], B["Cf"][:], F.Identity, bias=sm("cb"))
        count(2, 3)
        cp("IN0 IN1 IN2 IN3", "WI", B["WI"][:], B["IN"][:, :, 0:256:17])
        mms("WI BD", "PD2s", [(PD[2][:, 128:256], B["WI"][:], B["BD"][:], True, True)])
        count(3, 4)
        mms("fe I14 I14z", "PB5", [(KS[:, 0:256], B["fe"][:], B["I14"][:], False, True)])
        tt("PD2s Kc", "wr", B["wr"][:], PD[2][:, 128:256], B["Kc"][:, 128:256], A.is_gt)
        mms("nIh wr EQ0 EQ1", "PD0w", [(PD[0][:, 0:128], B["nIh"][:], B["wr"][:], True, False)]
            + [(PD[0][:, 16 * k:16 * k + 16], B["EQ"][:, 128 * k:128 * k + 128], B["wr"][:, 16 * k:16 * k + 16], False, False) for k in range(8)]
            + [(PD[0][:, 0:128], B["nIh"][:], B["wr"][:], False, True)])
        sK = KS[:, 128:256]
        tt("PB5 Kc", "cap", B["cap"][:], sK, B["Kc"][:, 0:128], A.is_gt)
        tt("PB5 cap", "scap", B["scap"][:], sK, B["cap"][:], A.mult)
        tt("PB5 Kc", "nc", B["nc"][:], sK, B["Kc"][:, 0:128], A.is_le)
        op("V", "Mh scap", "scs", lambda: V.tensor_tensor_scan(B["scs"][:], B["Mh"][:], B["scap"][:], 0.0, A.mult, A.max))
        for k in range(4):
            ts("P scs", "sp", B["sp"][:, 16 * k:16 * k + 16], B["P"][:, 0:16], B["scs"][:, 16 * k + 15:16 * k + 16], None, A.mult)
        tt("PB5 nc", "mk", B["mk"][:], KS[:, 0:128], B["nc"][:], A.mult)
        tt("PD0w TPm", "wP", B["wP"][:], PD[0][:, 0:128], B["TPm"][:], A.is_lt)
        op("V", "Mh mk", "sc", lambda: V.tensor_tensor_scan(B["sc"][:], B["Mh"][:], B["mk"][:], 0.0, A.mult, A.max))
        for k in range(8):
            ts("P sc", "zc", B["zc"][:, 16 * k:16 * k + 16], B["P"][:, 0:16], B["sc"][:, 16 * k + 15:16 * k + 16], None, A.mult)
        tt("wr PB7", "wd", B["wd"][:], B["wr"][:], CP, A.mult)
        mms("Id nId x yl%d" % t, "PB4d", [(U[:, 256:384], B["Id"][:], x, True, False), (U[:, 256:384], B["nId"][:], B["yl"][:, L * t:L * t + L], False, True)])
        act("PB4d", "nx", nx, U[:, 256:384], F.Abs)
        for k in range(4, 8):
            act("P scs", "sp4", B["sp"][:, 16 * k:16 * k + 16], B["P"][:, 0:16], F.Copy, scale=B["scs"][:, 16 * k + 15:16 * k + 16])
        act("PD0w", "wL", B["wL"][:], PD[0][:, 0:128], F.Relu, scale=-1.0)
        mms("IF evP Pn P128 Id", "PB6v", [(PB6[:, 0:128], B["IF"][:, 0:128], B["evP"][:], True, False), (PB6[:, 0:128], B["IF"][:, 0:128], B["Pn"][:], False, False)]
            + [(PB6[:, 0:128], B["Id"][:], B["P128"][:], False, False)] * t)
        mms("cap Id", "PD3c", [(PD[3][:, 0:128], B["cap"][:], B["Id"][:], True, True)])
        mms("sp sp4 I4", "PB6v", [(PB6[:, 0:128], B["sp"][:], B["I4"][:], False, True)])
        mms("wP CH2", "PD2l", [(PD[2][:, 0:16], B["wP"][:], B["CH2"][:], True, True)])
        mms("zc BDf", "PD2l", [(PD[2][:, 24:32], B["zc"][:], B["BDf"][:], True, True)])
        mms("wd CH2", "PD2l", [(PD[2][:, 16:24], B["wd"][:], B["CH2"][:, 0:8], True, True)])
        cp("PD2l", "ch1", sm("ch1"), PD[2][:, 24:32])
        ts("ch1", "ch2", sm("ch2"), sm("ch1"), 2047, None, A.bitwise_and)
        tt("e2 ch2", "ch3", sm("ch3"), vf, sm("ch2"), A.subtract)
        tt("PD2l ch3", "ch4", sm("ch4"), PD[2][:, 16:24], sm("ch3"), A.mult)
        tt("ch2 ch4", "BBb", B["BB"][:, 8:16], sm("ch2"), sm("ch4"), A.add)
        tt("PD3c AAb", "mmb", B["mm"][:, 128:256], PD[3][:, 0:128], B["AA"][:, 128:256], A.mult)
        tt("PB6v mmb", "VC", B["VC"][:], PB6[:, 0:128], B["mm"][:, 128:256], A.add)
        mms("LW nx", "PD1b", [(PD[1][:, 128:136], B["LW"][:, 128 * r:128 * r + 128], B["XX"][:, r:128:16], r == 0, r == 15) for r in range(16)])
        cp("PD1b", "bk1", sm("bk1"), PD[1][:, 128:136])
        ts("bk1", "bk2", sm("bk2"), sm("bk1"), R - 1, None, A.bitwise_and)
        tt("bk2 e2", "BWb", B["BW"][:, 8:16], sm("bk2"), vf, A.subtract)
        mms("Id nx x one CA", "PB4a", [(U[:, 0:256], B["Id"][:], B["XX"][:], True, False), (U[:, 0:256], B["one"][:], B["CA"][:], False, False)])
        mms("wL JJ", "PB4a", [(U[:, 0:256], B["wL"][:], B["JJ"][:], False, True)])
        mms("x Id one CA wL JJ", "PD1x", [(PD[1][:, 0:128], B["Id"][:], x, True, False), (PD[1][:, 0:128], B["one"][:], B["CA"][:, 0:128], False, False),
                                          (PD[1][:, 0:128], B["wL"][:], B["JJ"][:, 0:128], False, True)])
        mms("cap scap wL Id I4", "PB5n", [(KS[:, 0:128], B["cap"][:], B["Id"][:], True, True), (KS[:, 128:256], B["scap"][:], B["I4"][:], True, True),
                                          (KS[:, 256:384], B["wL"][:], B["Id"][:], True, True)])
        act("PB4a", "xm", B["xm"][:], U[:, 0:256], F.Relu)
        act("PD1x", "Xz X%d" % t, B["X"][:, M + L * t:M + L * t + L], PD[1][:, 0:128], F.Relu)
        if not last:
            mms("xm Id", "PB4y", [(U[:, 384:512], B["xm"][:, 0:128], B["Id"][:], True, False), (U[:, 384:512], B["xm"][:, 128:256], B["Id"][:], False, True)])
            act("PB4y", "xT", B["xT"][:], U[:, 384:512], F.Copy)
        else:
            newx()
        tt("PD2l BWa BWb", "e1", sm("e1"), PD[2][:, 0:16], B["BW"][:], A.mult)
        tt("e1 BBa BBb", "e2", B["e2"][:], sm("e1"), B["BB"][:], A.add)
        cp("e2", "lst", B["lst"][:], B["e2"][:])
        if not last:
            nodes_at(t + 1)
        if not last:
            op("V", "lst VC", ER, lambda wg=wg: V.tensor_copy(B["E"][:, 0:128 + wg].indirect(B["lst"][:, 0:8]), B["VC"][:]))
        else:
            op("V", "lst VC EF", "EF", lambda: V.tensor_copy(B["EF"][:, 0:128 + wg].indirect(B["lst"][:, 0:8]), B["VC"][:]))
            dma("Y", "EF", "", "out", T.ykids[:, 0:wg], B["EF"][:, 128:128 + wg])
            newcols(t)
            dma("Y", "EF%d" % t, "", "out", T.ykids[:, M + L * t:M + L * t + L], B["EF"][:, 128 + M + L * t:128 + M + L * t + L])
            dma("S", XR + " X%d" % t, "", "out", T.ynodes[:], B["X"][:, M:M + L * STEPS])
            dma("S", "x", "", "out", T.ycand[:], x)
            dma("S", "e2", "", "out", T.yspot[:], vf)
    def schedule():
        N = len(calls)
        WAKE, LOOK = TUNE["wake"], TUNE["look"]
        noise = np.random.RandomState(TUNE["seed"]).rand(N) * TUNE["noise"]
        succ = [[] for _ in range(N)]
        left = [len(c["pre"]) for c in calls]
        for c in calls:
            for m in c["pre"]:
                succ[m].append(c["n"])
        prio = [0.0] * N
        for n in range(N - 1, -1, -1):
            c = calls[n]
            prio[n] = c["dur"] + c["lat"] + max([prio[m] + (WAKE if calls[m]["pre"][n] else 0.0) for m in succ[n]] or [0.0])
        for n in range(N):
            prio[n] += float(noise[n])
        free, end, start, est = {}, [0.0] * N, [0.0] * N, {}
        for n in range(N):
            if not left[n]:
                est[n] = 0.0
        out = []
        while est:
            at = {n: max(e, free.get(calls[n]["eng"], 0.0)) for n, e in est.items()}
            lo = min(at.values())
            n = max((m for m in at if at[m] <= lo + LOOK), key=lambda m: (prio[m], -m))
            c = calls[n]
            start[n] = at[n]
            if c["eng"] != "A":
                free[c["eng"]] = at[n] + c["dur"]
            end[n] = at[n] + c["dur"] + c["lat"]
            del est[n]
            out.append(n)
            for m in succ[n]:
                left[m] -= 1
                if not left[m]:
                    est[m] = max(end[q] + WAKE if w else start[q] + calls[q]["dur"] for q, w in calls[m]["pre"].items())
        return out

    if "order" not in ORDERS:
        ORDERS["order"] = schedule()
    for n in ORDERS["order"]:
        c = calls[n]
        eng = c["eng"]
        if eng == "A":
            snap[c["tok"]] = {}
            continue
        wait(eng, [calls[m]["tok"] for m, w in c["pre"].items() if w])
        i = c["fn"]()
        if c["kind"] == "c":
            cnt[eng] += 1
            i.then_inc(T.sem["s" + eng], 1)
            c["tok"] = ("s" + eng, cnt[eng])
        if c["tok"]:
            snap[c["tok"]] = dict(known[eng])
    for t in range(STEPS):
        for s in ("qo", "yo"):
            g.wait_ge(T.sem[s + str(t)], neng)
    g.wait_ge(T.sem.wloc, neng * (NB - 1))
    wait("G", [("sV", cnt["V"]), ("sS", cnt["S"]), ("sP", cnt["P"]), ("sG", cnt["G"])] + [("d_" + k, n) for k, n in dcount.items()]
         + [("wrem", neng * (NB - 1))] + [(k + str(t), neng) for k in ("qa", "ya") for t in range(STEPS)])
